import numpy as np, ml_dtypes
CORES = [3,7,11,15,131,135,139,143]
N = 8
BF = ml_dtypes.bfloat16
def gentries(a):
    return np.ascontiguousarray(a.reshape(8, 16, -1).transpose(0, 2, 1)).reshape(8, -1)
def gtable(e):
    e = np.asarray(e); return np.ascontiguousarray(e.reshape(8, -1, 16).transpose(0, 2, 1)).reshape(128, -1).astype(np.int32)
R, A, J, W, Q, SH, RO = 64, 8, 3, 2048, 21, 3, 3
def parts(rng):
    amp = rng.choice(np.array([16, 32, 64, 128]), (N, 8, 1, 1))
    p = (amp * rng.random((N, 8, 16, W))).astype(np.int64)
    s = rng.integers(0, 1009, (N, 8, 1, W)) + rng.integers(0, 16, (N, 8, 16, W))
    c = rng.integers(0, W, (N, 8, R, Q)); nbr = rng.integers(0, N * R, (N, 8, J, R)); ge = rng.integers(0, W, (N, 8, J, R))
    return p, s, c, nbr, ge
def pack(p, s, c, nbr, ge):
    return {"pe": np.ascontiguousarray(p.reshape(N, 128, W)).astype(np.float32).astype(BF), "se": np.ascontiguousarray(s.reshape(N, 128, W)).astype(np.int32),
            "cand": np.ascontiguousarray(c.reshape(N, 8, R * Q)).astype(np.int32),
            "nb": np.stack([gtable(a.reshape(8, -1)) for a in nbr]), "geo": np.stack([gtable(a.reshape(8, -1)) for a in ge])}
def setup_inputs(rng):
    return pack(*parts(rng))
def ladder():
    o = [512 + 8 * (A - 1 - a) for a in range(A)]
    w = [0] * A
    for i in range(A // 2):
        w[(A - 1 + 2 * i) % A] = 512 - 8 * i; w[2 * i] = 200 + 8 * (A // 2 - 1 - i)
    o += w[:A - 1]
    h = 512 - 8 * (A // 2 - 1); ch = [(A - 3 + 3 * i) % A for i in range(A)]; m = ch.index(A - 2)
    for i in range(A): w[ch[i]] = h - (h - 200) * i // m if i < m else 200 - 8 * (i - m)
    return np.array(o + w[:A - 3] + [w[A - 1]])
def setup_inputs_most(rng):
    p, s, c, nbr, ge = parts(rng); o = ladder(); k = W // 1024
    for q in range(N):
        for g in range(8):
            pm = rng.permutation(W); lv = np.zeros(W, np.int64); lv[pm] = np.arange(W) // k
            s[q, g] = lv[None, :]; p[q, g] = rng.integers(0, 2, (16, W))
            v = rng.integers(0, 1024, (R, Q)); v[:, :len(o)] = o[None, :] + rng.integers(-100, 301, (R, 1))
            c[q, g] = pm[v * k + rng.integers(0, k, (R, Q))]
    far = 1 + rng.permutation(N) % (N - 1)
    nbr = ((np.arange(N) + far) % N * R)[:, None, None, None] + rng.integers(0, R, (N, 8, J, R))
    return pack(p, s, c, nbr, ge)
def setup_inputs_ties(rng):
    p, s, c, nbr, ge = parts(rng)
    p[:, ::2] = rng.integers(0, 128, (N, 4, 16, 1)); p[:, 1::2] = rng.integers(0, 2, (N, 4, 16, W))
    lv = rng.integers(0, 4, (N, 8, 1, W)); lv[:, 1::2] = rng.integers(0, 12, (N, 4, 1, W))
    lone = rng.integers(0, 64, (N, 8, 1, W)) == np.arange(16)[:, None]
    s = 1 + lv + rng.integers(0, 900, (N, 8, 16, 1)) - lone
    return pack(p, s, c, nbr, ge)
def setup_inputs_ends(rng):
    p, s, c, nbr, ge = parts(rng)
    c[:, ::2] = rng.choice(np.array([0, 1, W // 2 - 1, W - 5, W - 3, W - 1]), (N, 4, R, Q)); ge[:, ::2] = rng.choice(np.array([0, 1, W - 1]), (N, 4, J, R))
    s[:, ::2, :, 0] = 0; s[:, ::2, :, W - 1] = 1023; s[:, ::2, :, W // 2 - 1] = 500
    p[:, ::4] = 127 * rng.integers(0, 2, (N, 2, 16, W))
    own = np.arange(N)[:, None, None] * R
    nbr[:, 0] = own + np.arange(R)
    nbr[:, 1] = rng.choice(np.array([0, R - 1, (N - 1) * R, N * R - 1]), (N, J, R))
    nbr[:, 3] = rng.integers(0, N * R, (N, 1, R))
    nbr[:, 5] = (own + R) % (N * R) + rng.integers(0, R, (N, J, R))
    nbr[:, 7] = own + rng.integers(0, R, (N, J, R))
    return pack(p, s, c, nbr, ge)
def setup_inputs_still(rng):
    p, s, c, nbr, ge = parts(rng); o = rng.permutation(8); b, h = o[4], o[5]
    c[:, o[4:6], ::4] = 1 << SH; nbr[:, o[4:6]] = 4 * rng.integers(0, N * R // 4, (N, 2, J, R)); ge[:, o[4:6]] = 64 * rng.integers(0, W // 64, (N, 2, J, R))
    p[:, b] = np.tile(rng.integers(0, 128, (N, 16, 64)), (1, 1, W // 64))
    s[:, b] = rng.integers(127 * J, 1016, (N, 1, W)) - J * p[:, b] + rng.integers(0, 8, (N, 16, W))
    t = np.tile(np.argsort(rng.random((N, 1, 64)), axis=-1) & 1, (1, 1, W // 64)); one = np.arange(16)[:, None] == rng.integers(0, 16, (N, 1, 1))
    p[:, h] = np.where(one, 127 * (1 - t), np.tile(rng.integers(0, 128, (N, 16, 64)), (1, 1, W // 64)))
    s[:, h] = 127 * J - J * p[:, h] + np.where(one, rng.integers(0, 101, (N, 1, 1)) + rng.integers(0, 3, (N, 1, W)), rng.integers(0, 56, (N, 1, W)) + 64 * t + rng.integers(0, 8, (N, 16, W)))
    q = int(rng.integers(0, N)); p[q] = rng.integers(0, 128, (8, 16, W)); s[q] = s[q] >> 5
    p[:, o[0]] = rng.integers(0, 128, (N, 16, 1)); s[:, o[0]] = rng.integers(0, 1024, (N, 16, 1))
    lv = rng.integers(0, 1024, (N, 1, W)); p[:, o[1]] = rng.integers(0, 2, (N, 16, W)); s[:, o[1]] = lv; s[:, o[1], int(rng.integers(0, 16))] = 1023 - lv[:, 0]
    for a in range(N):
        for g, sign in ((o[2], 1), (o[3], -1)):
            i = np.argsort(sign * s[a, g, 0][c[a, g]], axis=-1); c[a, g] = np.take_along_axis(c[a, g], i, -1)
    return pack(p, s, c, nbr, ge)
def setup_inputs_spread(rng):
    p, s, c, nbr, ge = parts(rng)
    p = np.minimum((np.exp2(7 * rng.random((N, 8, 1, W))) * rng.random((N, 8, 16, W))).astype(np.int64), 127)
    s = np.minimum((np.exp2(10 * rng.random((N, 8, 1, W))) * (0.875 + 0.125 * rng.random((N, 8, 16, W)))).astype(np.int64), 1023)
    e = rng.choice(np.array([1.0, 2.0, 4.0]), (N, 8, 1, 1))
    c = np.minimum((W * rng.random((N, 8, R, Q)) ** e).astype(np.int64), W - 1)
    nbr = np.minimum((N * R * rng.random((N, 8, J, R)) ** 2).astype(np.int64), N * R - 1)
    ge = np.minimum((W * rng.random((N, 8, J, R)) ** e).astype(np.int64), W - 1)
    return pack(p, s, c, nbr, ge)
def check_inputs(d):
    bad = []
    v = np.asarray(d["pe"]).astype(np.float32)
    if not (np.all(v >= 0) and np.all(v <= 127) and np.all(v == np.floor(v))): bad.append("range of pe")
    for k, hi in (("se", 1023), ("cand", W - 1), ("nb", N * R - 1), ("geo", W - 1)):
        if np.min(d[k]) < 0 or np.max(d[k]) > hi: bad.append("range of " + k)
    return bad
def reference(pe, se, cand, nb, geo):
    p = pe.astype(np.float32).astype(np.int32).reshape(N, 8, 16, W); s = se.astype(np.int32).reshape(N, 8, 16, W)
    qu = cand.astype(np.int64).reshape(N, 8, R, Q)
    nbl = np.stack([gentries(a) for a in nb]).astype(np.int64).reshape(N, 8, J, R); ge = np.stack([gentries(a) for a in geo]).astype(np.int64).reshape(N, 8, J, R)
    pos = np.zeros((N, 8, R, A), np.int64) + np.arange(A); head = np.full((N, 8, R, 1), A, np.int64)
    for t in range(RO):
        c = np.take_along_axis(qu, pos, 3)
        every = c.transpose(1, 0, 2, 3).reshape(8, N * R, A)
        gap = []
        for a in range(N):
            cu = every[np.arange(8)[:, None, None], nbl[a]]
            ix = (((c[a][:, None, :, :, None] * cu[:, :, :, None, :]) >> SH) + ge[a][:, :, :, None, None]) & (W - 1)
            e = np.take_along_axis(p[a], ix.reshape(8, 1, -1), 2).reshape(8, 16, J, R, A, A)
            low = np.min(e - np.roll(e, -(t + 1), axis=4), axis=5)
            own = np.take_along_axis(s[a], c[a].reshape(8, 1, -1), 2).reshape(8, 16, R, A)
            gap.append(own - np.roll(own, -(t + 1), axis=3) + np.add.reduce(low, axis=2))
        gap = np.stack(gap)
        dead = np.all(gap > 0, axis=2)
        if t < RO - 1:
            n = dead.astype(np.int64); upto = np.add.accumulate(n, axis=3)
            pos = np.where(dead, head + upto - n, pos); head = head + upto[..., -1:]
    return {"yc": np.where(dead, -1, c).reshape(N, 8, R * A).astype(np.float32), "yg": gap.reshape(N, 128, R * A).astype(np.float32)}

@@ -1,0 +1,437 @@
+from concourse.bass import DstId, RemoteDMATransfer
+from concourse.mybir import AluOpType as OP, ActivationFunctionType as AF
+
+CD = "float16"
+BF, F32, I32, U16 = "bfloat16", "float32", "int32", "uint16"
+
+SCRATCH = {}
+for _dt, _bufs in (
+        (I32, {"candi": [32, 21], "nbi": [12, 4], "nbs": [12, 2], "nbr": [6, 8], "ghl": [24], "i64": [64], "pcol": [4], "ah": [4],
+               "y1": [384], "y2": [384], "sew0": [2048], "sew1": [2048]}),
+        (CD, {"candf": [672], "cand8": [32, 8], "hd0": [16], "hd1": [16], "hd2": [16], "call0": [256], "call1": [256],
+              "sev0": [256], "sev1": [256]}),
+        (U16, {"nbl": [48], "ghu": [24], "lst0": [16], "lst": [16], "sel0": [16], "sel1": [16], "idx0": [384], "idx1": [384]}),
+        (F32, {"ghi": [192], "glo": [192], "geo8": [6, 128], "cols": [8], "win": [3072], "cu": [384], "adr0": [16], "adr1": [16],
+               "adr2": [16], "cw0": [672], "cw1": [672], "ygs0": [256], "ygs1": [256], "ycs0": [256], "ycs1": [256]}),
+        (BF, {"ones": [128], "big": [128], "z0": [544], "r0": [256], "zz": [272], "bc": [144], "bs": [144], "idn": [128],
+              "neg": [128], "dh0": [128], "dh1": [128], "one8": [128], "ltri": [128], "o16": [128], "rst": [1024], "ind": [256],
+              "dead": [16], "pew0": [2048], "pew1": [2048], "ee0": [6144], "ee1": [6144], "mm0": [6144], "mm1": [6144]})):
+    for _k in _bufs:
+        SCRATCH[_k] = ("sbuf", [128] + _bufs[_k], _dt)
+for _k, _n in (("psd0", 1024), ("psd1", 1024), ("psd2", 1024), ("psg", 512), ("psm", 512)):
+    SCRATCH[_k] = ("psum", [128, _n], F32)
+
+SEMAPHORES = (["cv", "cs", "cp", "cg", "dcand", "dtab", "dpe0", "dpe1", "dse0", "dse1", "dog0", "dog1", "doc0", "doc1"]
+              + ["arr%d" % n for n in range(6)] + ["snt%d" % n for n in range(6)])
+
+O_PR, O_C2, O_L1, O_CNT, O_PRE, O_HD, O_SEL = 0, 384, 384, 448, 464, 480, 496
+GATHERS = [(0, 2), (2, 2), (4, 2), (6, 2), (8, 2), (10, 1), (11, 1)]
+DIFFS = [(0, 1), (1, 2), (3, 2), (5, 2), (7, 2), (9, 1), (10, 2)]
+ORDER = {
+    0: "g1 x1 y1 z1 c2 g2 G0 G5 g3 cu0 g4 d0 d1 m0 m1 p0 d2 x0 m2 d3 y0 g6 m3 z0 d4 m4 d5 cu1 p1 m5 d6 self m6 gapf",
+    1: "gapl g0 x1 cnt y1 g1 z1 dead d0 fill l1 d1 g2 self g3 m0 m1 d2 g4 d3 m2 g5 g6 m3 cu0 head cu1 d4 m4 sel d5 m5 c2 "
+       "p0 x0 y0 z0 d6 gapf p1 m6",
+    5: "gapl x1 self y1 g0 d0 alive z1 g1 m0 G3 d1 g2 m1 g4 d2 g5 d3 d4 res g6 m2 m3 d5 m4 d6 m5 m6 gapf",
+}
+
+
+def slot_at(t, i, h):
+    s = t + 1
+    if s % 2 == 0:
+        return 2 * i + h
+    return (s * ((i + 3) % 4 + 4 * h)) % 8
+
+
+def rank_program(g, core, T, topo):
+    rank = T.rank_of(core)
+    if rank is None:
+        return
+    Q = {"v": g.vector, "s": g.scalar, "p": g.tensor, "g": g, "y": g.sync}
+    own = {"v": "cv", "s": "cs", "p": "cp", "g": "cg"}
+    total = {}
+    seen = {q: {} for q in Q}
+    wr, rd, bank = {}, {}, {}
+
+    def need(q, tok):
+        sem, val = tok[0], tok[1]
+        if seen[q].get(sem, 0) < val:
+            Q[q].wait_ge(T.sem[sem], val)
+            seen[q][sem] = val
+
+    def deps(q, reads, writes, banks):
+        want = {}
+        toks = [wr[k] for k in reads]
+        for k in writes:
+            toks += ([wr[k]] if k in wr else []) + rd.get(k, [])
+        toks = [t for t in toks if not (q == "p" and t[2] == "p")]
+        toks += [bank[k] for k in banks if k in bank and bank[k][2] != q]
+        for t in toks:
+            want[t[0]] = max(want.get(t[0], 0), t[1])
+        for sem in want:
+            need(q, (sem, want[sem]))
+
+    def note(tok, reads, writes, banks):
+        for k in reads:
+            rd.setdefault(k, []).append(tok)
+        for k in writes:
+            wr[k] = tok
+            rd[k] = []
+        for k in banks:
+            bank[k] = tok
+
+    def op(q, fn, reads=(), writes=(), banks=()):
+        deps(q, reads, writes, banks)
+        sem = own[q]
+        total[sem] = total.get(sem, 0) + 1
+        fn().then_inc(T.sem[sem], 1)
+        note((sem, total[sem], q), reads, writes, banks)
+
+    def dmas(sem, items, reads=(), writes=()):
+        for q, o, i in items:
+            deps(q, reads, writes, ())
+            Q[q].dma_start(o, i).then_inc(T.sem[sem], 16)
+        total[sem] = total.get(sem, 0) + 16 * len(items)
+        note((sem, total[sem], "dma"), reads, writes, ())
+
+    def mms(items, start=True, stop=True):
+        last = None
+        for grp in items:
+            for i, (o, l, r) in enumerate(grp):
+                last = g.tensor.matmul(o, l, r, start and i == 0, stop and i == len(grp) - 1)
+        return last
+
+    def select(out, src, pattern, cmp, fill, base, step, reads, writes):
+        op("g", lambda: g.affine_select(out, src, pattern, cmp, fill, base, step), reads, writes)
+
+    V, S = g.vector, g.scalar
+    psd = [T.psd0, T.psd1, T.psd2]
+    ring = [0]
+
+    others = [c for c in T.cores if c != core]
+    near = [c for c in others if c in topo.cores_of(core)]
+    far = [c for c in others if c not in near]
+
+    def engines_for(src):
+        o = [c for c in T.cores if c != src]
+        nr = [c for c in o if c in topo.cores_of(src)]
+        fr = [c for c in o if c not in nr]
+        fe = [e for e in topo.engines(src, fr[0]) if all(e in topo.engines(src, c) for c in fr)]
+        ne = [e for e in topo.engines(src, nr[0]) if e not in fe][0:4:2]
+        return fe, ne
+
+    def arrivals():
+        n = 0
+        for c in others:
+            fe, ne = engines_for(c)
+            n += len(ne) if c in near else len(fe)
+        return n
+
+    def send(n):
+        piece = T.win[:, 512 * n + 64 * rank:512 * n + 64 * rank + 64]
+        deps("g", ["own%d" % n], [], ())
+        fe, ne = engines_for(core)
+        trs = []
+        for dsts, es in ((far, fe), (near, ne)):
+            ids = []
+            for c in dsts:
+                rid, pid = topo.addr(c, core)
+                ids.append(DstId(rid=rid, pnc=pid))
+            trs.append(RemoteDMATransfer(dst_ids=ids, dma_engine_mask=sum(1 << e for e in es), remote_sem=T.sem["arr%d" % n],
+                                         srcs=[piece], dsts=[piece] * len(dsts)))
+        g.remote_dma_fused(trs, local_sem=T.sem["snt%d" % n])
+        total["snt%d" % n] = len(fe) + len(ne)
+        total["arr%d" % n] = arrivals()
+        wr["far%d" % n] = ("arr%d" % n, total["arr%d" % n], "dma")
+        wr["sent%d" % n] = ("snt%d" % n, total["snt%d" % n], "dma")
+
+    dmas("dcand", [("y", T.candi[0:16, :, :], T.cand[:])], writes=["candi"])
+    dmas("dtab", [("ys"[t], T.nbi[64 * b:64 * b + 64, 6 * t + 3 * f:6 * t + 3 * f + 3, :], (T.nb, T.geo)[t][64 * f:64 * f + 64, :])
+                  for t in (0, 1) for f in (0, 1) for b in (0, 1)], writes=["nbi"])
+    dmas("dpe0", [("ys"[b], T.pew0[64 * b:64 * b + 64, :], T.pe[0:64, :]) for b in (0, 1)], writes=["pew0"])
+
+    op("v", lambda: V.memset(T.ones[:], 1.0), writes=["ones"])
+    op("v", lambda: V.memset(T.z0[0:32, :], 0.0), writes=["z0"])
+    op("v", lambda: V.memset(T.bs[:], 0.0), writes=["bs"])
+    op("g", lambda: g.iota(T.pcol[:, 0:1], [[0, 1]], 0, 1), writes=["pcol"])
+    op("g", lambda: g.iota(T.i64[:], [[1, 64]], 0, 0), writes=["i64"])
+    for i in range(4):
+        select(T.z0[0:16, 136 * i + 7:136 * i + 135:8], T.ones[0:16, 0:16], [[0, 2], [-2, 4], [0, 2]], OP.is_equal, 0.0,
+               -(8 * (i // 2) + i % 2), 1, ["ones", "z0"], ["z0_%d" % i])
+    select(T.idn[:], T.ones[:], [[-1, 128]], OP.is_equal, 0.0, 0, 1, ["ones"], ["idn"])
+    for f in (0, 1):
+        select(T.r0[0:16, 128 * f:128 * f + 128], T.ones[0:16, :], [[-1, 2], [-2, 4], [0, 16]], OP.is_equal, 0.0, -8 * f, 1,
+               ["ones"], ["r0_%d" % f])
+    op("v", lambda: V.memset(T.zz[:], 0.0), writes=["zz"])
+    op("v", lambda: V.memset(T.bc[:], 0.0), writes=["bc"])
+    op("v", lambda: V.memset(T.big[:], 4096.0), writes=["big"])
+    op("v", lambda: V.tensor_scalar(T.ah[:, 0:1], T.pcol[:, 0:1], 7, None, OP.bitwise_and), ["pcol"], ["ah0"])
+    op("v", lambda: V.tensor_scalar(T.ah[:, 1:2], T.pcol[:, 0:1], 3, 1, OP.arith_shift_right, OP.bitwise_and), ["pcol"], ["ah1"])
+    op("v", lambda: V.memset(T.rst[:], 0.0), writes=["rst"])
+    op("v", lambda: V.tensor_copy(T.cols[:, 0:2], T.ah[:, 0:2]), ["ah0", "ah1"], ["c01"])
+
+    op("v", lambda: V.tensor_copy(T.cand8[0:16, :, :], T.candi[0:16, :, 0:8]), ["candi"], ["cand8"])
+
+    def first_l1(f):
+        op("p", lambda: mms([[(T.psm[:, O_L1 + 32 * b:O_L1 + 32 * b + 32],
+                               T.z0[0:16, 136 * (2 * f + b) + 7 - u:136 * (2 * f + b) + 135 - u], T.cand8[0:16, :, u])
+                              for u in range(8)] for b in (0, 1)]),
+           ["cand8", "z0_%d" % (2 * f), "z0_%d" % (2 * f + 1)], ["l1"], ["m"])
+
+    def l1_out(n):
+        op("v", lambda: V.tensor_copy(T.win[:, 512 * n + 64 * rank:512 * n + 64 * rank + 64], T.psm[:, O_L1:O_L1 + 64]),
+           ["l1"], ["own%d" % n], ["m"])
+        send(n)
+
+    first_l1(0)
+    op("v", lambda: V.tensor_scalar(T.cols[:, 2:3], T.cols[:, 1:2], -1.0, 1.0, OP.mult, OP.add), ["c01"], ["c2c"])
+    op("v", lambda: V.tensor_scalar(T.cols[:, 3:4], T.cols[:, 1:2], 21.0, T.cols[:, 0:1], OP.mult, OP.add), ["c01"], ["c3"])
+    op("v", lambda: V.tensor_scalar(T.cols[:, 4:5], T.cols[:, 1:2], 21.0, 8.0 - 1024.0, OP.mult, OP.add), ["c01"], ["c4"])
+    l1_out(0)
+    first_l1(1)
+    op("v", lambda: V.tensor_copy(T.candf[0:16, :], T.candi[0:16, :, :]), ["candi"], ["candf"])
+    l1_out(1)
+
+    def queue_window(f):
+        d = psd[f]
+        op("p", lambda: mms([[(d[:, 0:512], T.r0[0:16, 128 * f:128 * f + 128], T.candf[0:16, 0:512])],
+                             [(d[:, 512:672], T.r0[0:16, 128 * f:128 * f + 128], T.candf[0:16, 512:672])]]),
+           ["candf", "r0_%d" % f], ["d%d" % f], ["d%d" % f])
+        op("s", lambda: S.activation(T["cw%d" % f][:], d[:, 0:672], AF.Copy), ["d%d" % f], ["cw%d" % f], ["d%d" % f])
+
+    queue_window(0)
+    queue_window(1)
+
+    deps("y", ["sent0"], [], ())
+    dmas("dse0", [("y", T.sew0[64 * b:64 * b + 64, :], T.se[0:64, :]) for b in (0, 1)], writes=["sew0"])
+    dmas("dpe1", [("y", T.pew1[64 * b:64 * b + 64, :], T.pe[64:128, :]) for b in (0, 1)], writes=["pew1"])
+    dmas("dse1", [("y", T.sew1[64 * b:64 * b + 64, :], T.se[64:128, :]) for b in (0, 1)], writes=["sew1"])
+
+    select(T.bs[:, 15:143:16], T.ones[:, 0:8], [[-16, 8]], OP.is_equal, 0.0, 0, 1, ["ones", "bs"], ["bs1"])
+    for b in (0, 1):
+        select(T.zz[:, 136 * b + 7:136 * b + 135:8], T.ones[:, 0:16], [[0, 2], [-16, 4], [0, 2]], OP.is_equal, 0.0, -64 * b, 1,
+               ["ones", "zz"], ["zz%d" % b])
+    select(T.bc[:, 15:143:16], T.ones[:, 0:8], [[-16, 8]], OP.is_ge, 0.0, 0, 1, ["ones", "bc"], ["bc1"])
+    select(T.bc[:, 15:143:16], T.bc[:, 15:143:16], [[16, 8]], OP.is_ge, 0.0, 15, -1, ["bc1"], ["bc1"])
+    select(T.one8[:], T.ones[:], [[-8, 16], [0, 8]], OP.is_ge, 0.0, 0, 1, ["ones"], ["one8"])
+    select(T.one8[:], T.one8[:], [[8, 16], [0, 8]], OP.is_ge, 0.0, 7, -1, ["one8"], ["one8"])
+    select(T.ltri[:], T.one8[:], [[1, 128]], OP.is_gt, 0.0, 0, -1, ["one8"], ["ltri"])
+    select(T.ltri[:], T.ltri[:], [[1, 128]], OP.not_equal, 1024.0, 0, -1, ["ltri"], ["ltri"])
+    select(T.o16[:], T.big[:], [[-16, 8], [0, 16]], OP.is_ge, 0.0, 0, 1, ["big"], ["o16"])
+    select(T.o16[:], T.o16[:], [[16, 8], [0, 16]], OP.is_ge, 0.0, 15, -1, ["o16"], ["o16"])
+
+    for b in (0, 1):
+        op("v", lambda: V.tensor_copy(T.nbs[64 * b:64 * b + 64, :, :], T.nbi[64 * b:64 * b + 64, :, 2 * b:2 * b + 2]), ["nbi"], ["nbs%d" % b])
+    nbs = ["nbs0", "nbs1"]
+    op("v", lambda: V.tensor_scalar(T.lst0[:], T.i64[:, 0:16], 42.0, T.cols[:, 3:4], OP.mult, OP.add), ["i64", "c3"], ["lst0"])
+    op("v", lambda: V.tensor_scalar(T.ghl[:, 0:12], T.nbs[:, 6:12, :], 6, None, OP.arith_shift_right), nbs, ["gh"])
+    op("v", lambda: V.tensor_scalar(T.ghl[:, 12:24], T.nbs[:, 6:12, :], 63, None, OP.bitwise_and), nbs, ["gl"])
+    op("v", lambda: V.tensor_scalar(T.dh0[:], T.idn[:], T.cols[:, 2:3], None, OP.mult), ["idn", "c2c"], ["dh0"])
+    op("v", lambda: V.tensor_copy(T.ghu[:], T.ghl[:]), ["gh", "gl"], ["ghu"])
+    op("v", lambda: V.tensor_scalar(T.dh1[:], T.idn[:], T.cols[:, 1:2], None, OP.mult), ["idn", "c01"], ["dh1"])
+    op("v", lambda: V.tensor_scalar(T.ghi[:], T.i64[:, 0:64].indirect(T.ghu[:, 0:12]), 64.0, None, OP.mult), ["i64", "ghu"], ["ghi"])
+    for i in range(4):
+        op("v", lambda: V.tensor_copy(T.nbr[:, :, 2 * i:2 * i + 2], T.nbs[:, 0:6, :]), nbs, ["nbr%d" % i])
+    op("v", lambda: V.tensor_tensor(T.glo[:], T.i64[:, 0:64].indirect(T.ghu[:, 12:24]), T.ghi[:], OP.add), ["i64", "ghu", "ghi"], ["glo"])
+    op("v", lambda: V.tensor_copy(T.nbl[:], T.nbr[:]), ["nbr0", "nbr1", "nbr2", "nbr3"], ["nbl"])
+    op("v", lambda: V.memset(T.rst[:, 0:1024:8], 256.0), ["rst"], ["rst"])
+    for i in range(4):
+        op("s", lambda: S.activation(T.geo8[:, :, 32 * i:32 * i + 32], T.glo[:], AF.Copy, scale=8.0), ["glo"], ["geo8_%d" % i])
+    geo8 = ["geo8_%d" % i for i in range(4)]
+
+    def codes(f, lst, key):
+        op("v", lambda: V.tensor_copy(T["call%d" % f][:], T["cw%d" % f][:, 0:672].indirect(lst[:, 0:16])),
+           ["cw%d" % f, key], ["call%d" % f])
+
+    def c2(n):
+        cl = T["call%d" % (n % 2)]
+        op("p", lambda: mms([[(T.psm[:, O_C2 + 32 * i:O_C2 + 32 * i + 32], (T.dh0, T.dh1)[h][:], cl[:, slot_at(n // 2, i, h):256:8])
+                              for h in (0, 1)] for i in range(4)]), ["call%d" % (n % 2), "dh0", "dh1"], ["c2"], ["m"])
+
+    def se_list(f):
+        cl = T["call%d" % f]
+        op("p", lambda: mms([[(T.psm[:, O_SEL:O_SEL + 16], T.bs[:, 15 - q:143 - q], cl[:, q:256:16]) for q in range(16)]]),
+           ["call%d" % f, "bs1"], ["selp"], ["m"])
+        op("v", lambda: V.tensor_copy(T["sel%d" % f][:], T.psm[:, O_SEL:O_SEL + 16]), ["selp"], ["sel%d" % f], ["m"])
+
+    codes(0, T.lst0, "lst0")
+    op("v", lambda: V.tensor_scalar(T.neg[:], T.idn[:], -1.0, None, OP.mult), ["idn"], ["neg"])
+    codes(1, T.lst0, "lst0")
+    se_list(0)
+    op("v", lambda: V.tensor_scalar(T.adr0[:], T.i64[:, 0:16], 42.0, T.cols[:, 3:4], OP.mult, OP.add), ["i64", "c3"], ["adr0"])
+    op("v", lambda: V.tensor_scalar(T.hd0[:], T.i64[:, 0:16], 42.0, T.cols[:, 4:5], OP.mult, OP.add), ["i64", "c4"], ["hd0"])
+    se_list(1)
+    c2(0)
+
+    def neigh(n, j0, j1):
+        f = n % 2
+        op("s", lambda: S.activation(T.cu[:, 128 * j0:128 * j1],
+                                     T.win[:, 512 * n:512 * n + 512].indirect(T.nbl[:, 24 * f + 8 * j0:24 * f + 8 * j1]), AF.Copy),
+           ["own%d" % n, "far%d" % n, "nbl"], ["cu%d" % j for j in range(j0, j1)])
+
+    def products(n, j0, j1):
+        for j in range(j0, j1):
+            op("v", lambda: V.tensor_tensor(T.psm[:, O_PR + 128 * j:O_PR + 128 * j + 128], T.cu[:, 128 * j:128 * j + 128],
+                                            T.psm[:, O_C2:O_C2 + 128], OP.mult), ["cu%d" % j, "c2"], ["pr%d" % j], ["m"])
+
+    def shifted(n, j0, j1):
+        f = n % 2
+        op("v", lambda: V.tensor_tensor(T.y1[:, 128 * j0:128 * j1], T.psm[:, O_PR + 128 * j0:O_PR + 128 * j1],
+                                        T.geo8[:, 3 * f + j0:3 * f + j1, :], OP.add),
+           ["pr%d" % j for j in range(j0, j1)] + geo8, ["y1_%d" % j0], ["m"])
+
+    def wrapped(n, j0, j1):
+        op("v", lambda: V.tensor_scalar(T.y2[:, 128 * j0:128 * j1], T.y1[:, 128 * j0:128 * j1], 3, 2047, OP.arith_shift_right,
+                                        OP.bitwise_and), ["y1_%d" % j0], ["y2_%d" % j0])
+
+    def offsets(n, j0, j1):
+        f = n % 2
+        op("v", lambda: V.tensor_copy(T["idx%d" % f][:, 128 * j0:128 * j1], T.y2[:, 128 * j0:128 * j1]), ["y2_%d" % j0],
+           ["idx%d_%d" % (f, j) for j in range(j0, j1)])
+
+    def gather(n, k, q):
+        f = n % 2
+        x, c = GATHERS[k]
+        src = T["pew%d" % f][:, 0:2048].indirect(T["idx%d" % f][:, 32 * x:32 * (x + c)])
+        out = T["ee%d" % f][:, 512 * x:512 * (x + c)]
+        r, w = ["pew%d" % f, "idx%d_%d" % (f, x // 4)], ["e%d_%d" % (f, y) for y in range(x, x + c)]
+        if q == "v":
+            op("v", lambda: V.tensor_copy(out, src), r, w)
+        else:
+            op("s", lambda: S.activation(out, src, AF.Copy), r, w)
+
+    where = {}
+
+    def diff(n, k):
+        f = n % 2
+        i = ring[0] % 3
+        ring[0] += 1
+        where[n, k] = i
+        d, e = psd[i], T["ee%d" % f]
+        grps, r = [], []
+        x, c = DIFFS[k]
+        for y in range(x, x + c):
+            lo, z = 512 * (y - x), 4 * (y // 4) + (y + 1) % 4
+            r += ["e%d_%d" % (f, y), "e%d_%d" % (f, z)]
+            grp = [(d[:, lo:lo + 512], T.idn[:], e[:, 512 * y:512 * y + 512])]
+            if y % 4 == 0 and n // 2 != 1:
+                grp += [(d[:, lo + q:lo + 512:16], T.neg[:], e[:, 512 * z + (q + 8) % 16:512 * z + 512:16]) for q in range(16)]
+            else:
+                grp.append((d[:, lo:lo + 512], T.neg[:], e[:, 512 * z:512 * z + 512]))
+            grps.append(grp)
+        op("p", lambda: mms(grps), r + ["idn", "neg"], ["d%d" % i], ["d%d" % i])
+
+    def least(n, k):
+        f, i = n % 2, where[n, k]
+        x, c = DIFFS[k]
+        op("v", lambda: V.tensor_tensor_scan(T["mm%d" % f][:, 512 * x:512 * (x + c)], T.rst[:, 0:512 * c], psd[i][:, 0:512 * c], 0.0,
+                                             OP.add, OP.min), ["d%d" % i, "rst"], ["m%d_%d" % (f, y) for y in range(x, x + c)], ["d%d" % i])
+
+    def selfs(n):
+        f = n % 2
+        op("v", lambda: V.tensor_copy(T["sev%d" % f][:], T["sew%d" % f][:, 0:2048].indirect(T["sel%d" % f][:, 0:16])),
+           ["sew%d" % f, "sel%d" % f], ["sev%d" % f])
+
+    G = T.psg
+    places = [(i, h) for i in range(4) for h in (0, 1)]
+
+    def sums(n, j):
+        m = T["mm%d" % (n % 2)]
+        if n < 4:
+            return [(G[:, 0:256], T.idn[:], m[:, 2048 * j + 7:2048 * j + 2048:8])]
+        return [(G[:, slot_at(2, i, h):256:8], T.idn[:], m[:, 2048 * j + 512 * i + 8 * h + 7:2048 * j + 512 * i + 512:16]) for i, h in places]
+
+    def gap_first(n):
+        f, t = n % 2, n // 2
+        v = T["sev%d" % f]
+        if n < 4:
+            grp = sums(n, 0)
+            for i, h in places:
+                a, o = slot_at(t, i, h), G[:, 64 * i + h:64 * i + 64:2]
+                grp += [(o, T.idn[:], v[:, a:256:8]), (o, T.neg[:], v[:, (a + t + 1) % 8:256:8])]
+        else:
+            grp = [(G[:, 0:256], T.idn[:], v[:])] + [(G[:, a:256:8], T.neg[:], v[:, (a + 3) % 8:256:8]) for a in range(8)] + sums(n, 0)
+        op("p", lambda: mms([grp + sums(n, 1)], stop=False), ["sev%d" % f, "idn", "neg"] + ["m%d_%d" % (f, y) for y in range(8)], ["gap"], ["g"])
+
+    def gap_last(n):
+        op("p", lambda: mms([sums(n, 2)], start=False), ["m%d_%d" % (n % 2, y) for y in range(8, 12)], ["gap"], ["g"])
+
+    def count(n):
+        at = {slot_at(n // 2, i, h): 64 * i + h for i, h in places}
+        op("v", lambda: V.tensor_scalar(T.ind[:], G[:, 0:256], 0.5, None, OP.is_gt), ["gap"], ["ind"], ["g"])
+        op("p", lambda: mms([[(T.psm[:, O_CNT:O_CNT + 16], T.bc[:, 15 - q:143 - q],
+                               T.ind[:, at[q % 8] + 2 * (q // 8):at[q % 8] - at[q % 8] % 64 + 64:4]) for q in range(16)]]),
+           ["ind", "bc1"], ["cnt"], ["m"])
+
+    def deaths(n):
+        f = n % 2
+        hd, key = (T.hd0, "hd0") if n < 2 else (T["hd%d" % (f + 1)], "hd%d" % (f + 1))
+        op("v", lambda: V.tensor_scalar(T.dead[:], T.psm[:, O_CNT:O_CNT + 16], 15.5, None, OP.is_gt), ["cnt"], ["dead"], ["m"])
+        op("p", lambda: mms([[(T.psm[:, O_PRE:O_PRE + 16], T.idn[:], hd[:]), (T.psm[:, O_PRE:O_PRE + 16], T.ltri[:], T.dead[:])]]),
+           ["dead", "ltri", key], ["pre"], ["m"])
+
+    def refill(n):
+        f = n % 2
+        ad, key = T["adr%d" % (f + 1)], "adr%d" % (f + 1)
+        old, okey = (T.adr0, "adr0") if n < 2 else (ad, key)
+        op("v", lambda: V.tensor_tensor(ad[:], T.psm[:, O_PRE:O_PRE + 16], old[:], OP.max), ["pre", okey], [key], ["m"])
+        op("v", lambda: V.tensor_copy(T.lst[:], ad[:]), [key], ["lst"])
+        codes(f, T.lst, "lst")
+        cl = T["call%d" % f]
+        op("p", lambda: mms([[(T.psm[:, O_L1 + 32 * b:O_L1 + 32 * b + 32], T.zz[:, 136 * b + 7 - u:136 * b + 135 - u],
+                               cl[:, u:256:8]) for u in range(8)] for b in (0, 1)]),
+           ["call%d" % f, "zz0", "zz1"], ["l1"], ["m"])
+
+    def heads(n):
+        f = n % 2
+        o = T.psm[:, O_HD:O_HD + 16]
+        op("p", lambda: mms([[(o, T.one8[:], T.dead[:]), (o, T.idn[:], T.hd0[:])]]), ["dead", "one8", "hd0"], ["hdp"], ["m"])
+        op("v", lambda: V.tensor_copy(T["hd%d" % (f + 1)][:], o), ["hdp"], ["hd%d" % (f + 1)], ["m"])
+
+    def alive(n):
+        op("v", lambda: V.tensor_scalar(T.ind[:], G[:, 0:256], 0.5, 2.0 ** -16, OP.is_lt, OP.subtract), ["gap"], ["ind"], ["g"])
+        op("p", lambda: g.tensor.matmul(T.psm[:, 0:256], T.o16[:], T.ind[:], True, True), ["ind", "o16"], ["liv"], ["m"])
+
+    def results(n):
+        f = n % 2
+        yg, yc = T["ygs%d" % f], T["ycs%d" % f]
+        qs = "yy" if n == 4 else "ys"
+        op("v", lambda: V.tensor_copy(yg[:], G[:, 0:256]), ["gap"], ["ygs%d" % f], ["g"])
+        dmas("dog%d" % f, [(qs[b], T.yg[64 * f:64 * f + 64, 256 * b:256 * b + 256], yg[64 * b:64 * b + 64, :]) for b in (0, 1)],
+             reads=["ygs%d" % f])
+        op("v", lambda: V.tensor_tensor(yc[:], T.psm[:, 0:256], T["call%d" % f][:], OP.min), ["liv", "call%d" % f], ["ycs%d" % f], ["m"])
+        dmas("doc%d" % f, [(qs[b], T.yc[4 * f:4 * f + 4, 256 * b:256 * b + 256], yc[64 * b:64 * b + 64:16, :]) for b in (0, 1)],
+             reads=["ycs%d" % f])
+
+    neigh(0, 0, 1)
+    neigh(0, 1, 3)
+    for step in (products, shifted, wrapped, offsets):
+        step(0, 0, 1)
+    products(0, 1, 3)
+    for n in range(6):
+        p = n - 1
+        steps = {"gapl": lambda: gap_last(p), "cnt": lambda: count(p), "dead": lambda: deaths(p), "fill": lambda: refill(p),
+                 "l1": lambda: l1_out(n + 1), "sel": lambda: se_list(p % 2), "head": lambda: heads(p) if p < 2 else None,
+                 "c2": lambda: c2(n + 1), "self": lambda: selfs(n), "gapf": lambda: gap_first(n),
+                 "cu0": lambda: neigh(n + 1, 0, 1), "cu1": lambda: neigh(n + 1, 1, 3),
+                 "p0": lambda: products(n + 1, 0, 1), "x0": lambda: shifted(n + 1, 0, 1), "y0": lambda: wrapped(n + 1, 0, 1),
+                 "z0": lambda: offsets(n + 1, 0, 1), "p1": lambda: products(n + 1, 1, 3), "x1": lambda: shifted(n, 1, 3),
+                 "y1": lambda: wrapped(n, 1, 3), "z1": lambda: offsets(n, 1, 3),
+                 "alive": lambda: alive(p), "res": lambda: results(p)}
+        for w in ORDER.get(n, ORDER[1]).split():
+            if w in steps:
+                steps[w]()
+            elif w[0] == "g":
+                gather(n, int(w[1:]), "s")
+            elif w[0] == "G":
+                gather(n, int(w[1:]), "v")
+            elif w[0] == "d":
+                diff(n, int(w[1:]))
+            else:
+                least(n, int(w[1:]))
+    gap_last(5)
+    alive(5)
+    results(5)
+
+    for sem in total:
+        if max(seen[q].get(sem, 0) for q in Q) < total[sem]:
+            need("g", (sem, total[sem]))

@@ -6,40 +6,47 @@ BF, F32, I32, U16 = "bfloat16", "float32", "int32", "uint16"
 
 SCRATCH = {}
 for _dt, _bufs in (
-        (I32, {"candi": [32, 21], "nbi": [12, 4], "nbs": [12, 2], "nbr": [6, 8], "ghl": [24], "i64": [64], "pcol": [4], "ah": [4],
-               "y1": [384], "y2": [384], "sew0": [2048], "sew1": [2048]}),
+        (I32, {"candi": [32, 21], "nbi": [12, 4], "nbs": [12, 2], "ghl": [24], "i64": [64], "pcol": [4], "ah": [4],
+               "y0": [384], "y2": [384], "sew0": [2048], "sew1": [2048]}),
         (CD, {"candf": [672], "cand8": [32, 8], "hd0": [16], "hd1": [16], "hd2": [16], "call0": [256], "call1": [256],
-              "sev0": [256], "sev1": [256]}),
-        (U16, {"nbl": [48], "ghu": [24], "lst0": [16], "lst": [16], "sel0": [16], "sel1": [16], "idx0": [384], "idx1": [384]}),
-        (F32, {"ghi": [192], "glo": [192], "geo8": [6, 128], "cols": [8], "win": [3072], "cu": [384], "adr0": [16], "adr1": [16],
-               "adr2": [16], "cw0": [672], "cw1": [672], "ygs0": [256], "ygs1": [256], "ycs0": [256], "ycs1": [256]}),
+              "sev0": [256], "sev1": [256], "glo": [192]}),
+        (U16, {"nbl": [6, 8], "ghu": [24], "lst0": [16], "lst1": [16], "lst2": [16], "sel0": [16], "sel1": [16], "idx0": [384],
+               "idx1": [384]}),
+        (F32, {"ghi": [192], "cols": [8], "win": [3072], "c2s0": [128], "c2s1": [128], "cw0": [672], "cw1": [672],
+               "ygs0": [256], "ygs1": [256], "ycs0": [256], "ycs1": [256]}),
         (BF, {"ones": [128], "big": [128], "z0": [544], "r0": [256], "zz": [272], "bc": [144], "bs": [144], "idn": [128],
               "neg": [128], "dh0": [128], "dh1": [128], "one8": [128], "ltri": [128], "o16": [128], "rst": [1024], "ind": [256],
-              "dead": [16], "pew0": [2048], "pew1": [2048], "ee0": [6144], "ee1": [6144], "mm0": [6144], "mm1": [6144]})):
+              "dead": [16], "pew0": [4096], "pew1": [4096], "ee0": [6144], "ee1": [6144], "dd0": [6144],
+              "dd1": [6144], "mm0": [6144], "mm1": [6144]})):
     for _k in _bufs:
         SCRATCH[_k] = ("sbuf", [128] + _bufs[_k], _dt)
-for _k, _n in (("psd0", 1024), ("psd1", 1024), ("psd2", 1024), ("psg", 512), ("psm", 512)):
+for _k, _n in (("psd", 2048), ("psq", 1024), ("psg", 512), ("psm", 512)):
     SCRATCH[_k] = ("psum", [128, _n], F32)
 
 SEMAPHORES = (["cv", "cs", "cp", "cg", "dcand", "dtab", "dpe0", "dpe1", "dse0", "dse1", "dog0", "dog1", "doc0", "doc1"]
               + ["arr%d" % n for n in range(6)] + ["snt%d" % n for n in range(6)])
 
-O_PR, O_C2, O_L1, O_CNT, O_PRE, O_HD, O_SEL = 0, 384, 384, 448, 464, 480, 496
-GATHERS = [(0, 2), (2, 2), (4, 2), (6, 2), (8, 2), (10, 1), (11, 1)]
-DIFFS = [(0, 1), (1, 2), (3, 2), (5, 2), (7, 2), (9, 1), (10, 2)]
+O_C2, O_L1, O_CNT, O_PRE, O_HD, O_SEL = 256, 384, 448, 464, 480, 496
+PLACE = [2, 0, 1, 3]
+OWNER = [2, 3, 0, 1]
+RIVAL = [3, 2, 0, 1]
+DEAD_ON, SELF_ON, SELC_ON, CALL_ON = "v", "v", "v", "s"
 ORDER = {
-    0: "g1 x1 y1 z1 c2 g2 G0 G5 g3 cu0 g4 d0 d1 m0 m1 p0 d2 x0 m2 d3 y0 g6 m3 z0 d4 m4 d5 cu1 p1 m5 d6 self m6 gapf",
-    1: "gapl g0 x1 cnt y1 g1 z1 dead d0 fill l1 d1 g2 self g3 m0 m1 d2 g4 d3 m2 g5 g6 m3 cu0 head cu1 d4 m4 sel d5 m5 c2 "
-       "p0 x0 y0 z0 d6 gapf p1 m6",
-    5: "gapl x1 self y1 g0 d0 alive z1 g1 m0 G3 d1 g2 m1 g4 d2 g5 d3 d4 res g6 m2 m3 d5 m4 d6 m5 m6 gapf",
+    "all": "pre- fill- d03 alive- call- r20 f03 out- f13 l1- r22 f12 d02 d12 c2+ d20 e03 self e02 c2c+ d13 r23 head- m101 d22 m001 "
+           "m023 P20 r21 d21 e12 liv- p0+ p2+ e13 d23 y0+ p1+ z0+ yg- P22 headc- P21 m123 P23 s0 r001+ sel+ s1 s2 y12+ selc+ ind "
+           "z12+ f02+ r11+ r10+ cnt yc- dead",
 }
 
 
-def slot_at(t, i, h):
-    s = t + 1
-    if s % 2 == 0:
+def slot_at(t, s, h):
+    i, step = PLACE[s], t + 1
+    if step % 2 == 0:
         return 2 * i + h
-    return (s * ((i + 3) % 4 + 4 * h)) % 8
+    return (step * ((i + 3) % 4 + 4 * h)) % 8
+
+
+def gap_cols(t, k, h, x0, dx):
+    return 64 * k + h + 2 * x0, 64 * k + 64, 2 * dx
 
 
 def rank_program(g, core, T, topo):
@@ -104,8 +111,9 @@ def rank_program(g, core, T, topo):
         op("g", lambda: g.affine_select(out, src, pattern, cmp, fill, base, step), reads, writes)
 
     V, S = g.vector, g.scalar
-    psd = [T.psd0, T.psd1, T.psd2]
-    ring = [0]
+
+    def move(q, o, i, reads, writes, banks=()):
+        op(q, lambda: V.tensor_copy(o, i) if q == "v" else S.activation(o, i, AF.Copy), reads, writes, banks)
 
     others = [c for c in T.cores if c != core]
     near = [c for c in others if c in topo.cores_of(core)]
@@ -147,7 +155,7 @@ def rank_program(g, core, T, topo):
     dmas("dcand", [("y", T.candi[0:16, :, :], T.cand[:])], writes=["candi"])
     dmas("dtab", [("ys"[t], T.nbi[64 * b:64 * b + 64, 6 * t + 3 * f:6 * t + 3 * f + 3, :], (T.nb, T.geo)[t][64 * f:64 * f + 64, :])
                   for t in (0, 1) for f in (0, 1) for b in (0, 1)], writes=["nbi"])
-    dmas("dpe0", [("ys"[b], T.pew0[64 * b:64 * b + 64, :], T.pe[0:64, :]) for b in (0, 1)], writes=["pew0"])
+    dmas("dpe0", [("ys"[b], T.pew0[64 * b:64 * b + 64, 0:2048], T.pe[0:64, :]) for b in (0, 1)], writes=["pe0"])
 
     op("v", lambda: V.memset(T.ones[:], 1.0), writes=["ones"])
     op("v", lambda: V.memset(T.z0[0:32, :], 0.0), writes=["z0"])
@@ -161,6 +169,7 @@ def rank_program(g, core, T, topo):
     for f in (0, 1):
         select(T.r0[0:16, 128 * f:128 * f + 128], T.ones[0:16, :], [[-1, 2], [-2, 4], [0, 16]], OP.is_equal, 0.0, -8 * f, 1,
                ["ones"], ["r0_%d" % f])
+    select(T.bs[:, 15:143:16], T.ones[:, 0:8], [[-16, 8]], OP.is_equal, 0.0, 0, 1, ["ones", "bs"], ["bs1"])
     op("v", lambda: V.memset(T.zz[:], 0.0), writes=["zz"])
     op("v", lambda: V.memset(T.bc[:], 0.0), writes=["bc"])
     op("v", lambda: V.memset(T.big[:], 4096.0), writes=["big"])
@@ -177,36 +186,37 @@ def rank_program(g, core, T, topo):
                               for u in range(8)] for b in (0, 1)]),
            ["cand8", "z0_%d" % (2 * f), "z0_%d" % (2 * f + 1)], ["l1"], ["m"])
 
-    def l1_out(n):
-        op("v", lambda: V.tensor_copy(T.win[:, 512 * n + 64 * rank:512 * n + 64 * rank + 64], T.psm[:, O_L1:O_L1 + 64]),
-           ["l1"], ["own%d" % n], ["m"])
+    def l1_out(n, q):
+        o, i = T.win[:, 512 * n + 64 * rank:512 * n + 64 * rank + 64], T.psm[:, O_L1:O_L1 + 64]
+        op(q, lambda: V.tensor_copy(o, i) if q == "v" else S.activation(o, i, AF.Copy), ["l1"], ["own%d" % n], ["m"])
         send(n)
 
+    move("s", T.candf[0:16, :], T.candi[0:16, :, :], ["candi"], ["candf"])
     first_l1(0)
     op("v", lambda: V.tensor_scalar(T.cols[:, 2:3], T.cols[:, 1:2], -1.0, 1.0, OP.mult, OP.add), ["c01"], ["c2c"])
     op("v", lambda: V.tensor_scalar(T.cols[:, 3:4], T.cols[:, 1:2], 21.0, T.cols[:, 0:1], OP.mult, OP.add), ["c01"], ["c3"])
     op("v", lambda: V.tensor_scalar(T.cols[:, 4:5], T.cols[:, 1:2], 21.0, 8.0 - 1024.0, OP.mult, OP.add), ["c01"], ["c4"])
-    l1_out(0)
+    l1_out(0, "s")
     first_l1(1)
-    op("v", lambda: V.tensor_copy(T.candf[0:16, :], T.candi[0:16, :, :]), ["candi"], ["candf"])
-    l1_out(1)
+    l1_out(1, "s")
 
     def queue_window(f):
-        d = psd[f]
+        d = T.psd[:, 1024 * f:1024 * f + 672]
+        bk = ["d%d" % (2 * f), "d%d" % (2 * f + 1)]
         op("p", lambda: mms([[(d[:, 0:512], T.r0[0:16, 128 * f:128 * f + 128], T.candf[0:16, 0:512])],
                              [(d[:, 512:672], T.r0[0:16, 128 * f:128 * f + 128], T.candf[0:16, 512:672])]]),
-           ["candf", "r0_%d" % f], ["d%d" % f], ["d%d" % f])
-        op("s", lambda: S.activation(T["cw%d" % f][:], d[:, 0:672], AF.Copy), ["d%d" % f], ["cw%d" % f], ["d%d" % f])
+           ["candf", "r0_%d" % f], bk, bk)
+        op("s", lambda: S.activation(T["cw%d" % f][:], d, AF.Copy), bk, ["cw%d" % f], bk)
 
     queue_window(0)
     queue_window(1)
 
     deps("y", ["sent0"], [], ())
     dmas("dse0", [("y", T.sew0[64 * b:64 * b + 64, :], T.se[0:64, :]) for b in (0, 1)], writes=["sew0"])
-    dmas("dpe1", [("y", T.pew1[64 * b:64 * b + 64, :], T.pe[64:128, :]) for b in (0, 1)], writes=["pew1"])
+    dmas("dpe1", [("y", T.pew1[64 * b:64 * b + 64, 2048 * i:2048 * i + 2048], T.pe[64:128, :]) for b in (0, 1) for i in (0, 1)],
+         writes=["pew1"])
     dmas("dse1", [("y", T.sew1[64 * b:64 * b + 64, :], T.se[64:128, :]) for b in (0, 1)], writes=["sew1"])
 
-    select(T.bs[:, 15:143:16], T.ones[:, 0:8], [[-16, 8]], OP.is_equal, 0.0, 0, 1, ["ones", "bs"], ["bs1"])
     for b in (0, 1):
         select(T.zz[:, 136 * b + 7:136 * b + 135:8], T.ones[:, 0:16], [[0, 2], [-16, 4], [0, 2]], OP.is_equal, 0.0, -64 * b, 1,
                ["ones", "zz"], ["zz%d" % b])
@@ -230,207 +240,240 @@ def rank_program(g, core, T, topo):
     op("v", lambda: V.tensor_scalar(T.dh1[:], T.idn[:], T.cols[:, 1:2], None, OP.mult), ["idn", "c01"], ["dh1"])
     op("v", lambda: V.tensor_scalar(T.ghi[:], T.i64[:, 0:64].indirect(T.ghu[:, 0:12]), 64.0, None, OP.mult), ["i64", "ghu"], ["ghi"])
     for i in range(4):
-        op("v", lambda: V.tensor_copy(T.nbr[:, :, 2 * i:2 * i + 2], T.nbs[:, 0:6, :]), nbs, ["nbr%d" % i])
+        op("v", lambda: V.tensor_copy(T.nbl[:, :, 2 * i:2 * i + 2], T.nbs[:, 0:6, :]), nbs, ["nbl%d" % i])
+    nbl = ["nbl%d" % i for i in range(4)]
     op("v", lambda: V.tensor_tensor(T.glo[:], T.i64[:, 0:64].indirect(T.ghu[:, 12:24]), T.ghi[:], OP.add), ["i64", "ghu", "ghi"], ["glo"])
-    op("v", lambda: V.tensor_copy(T.nbl[:], T.nbr[:]), ["nbr0", "nbr1", "nbr2", "nbr3"], ["nbl"])
-    op("v", lambda: V.memset(T.rst[:, 0:1024:8], 256.0), ["rst"], ["rst"])
-    for i in range(4):
-        op("s", lambda: S.activation(T.geo8[:, :, 32 * i:32 * i + 32], T.glo[:], AF.Copy, scale=8.0), ["glo"], ["geo8_%d" % i])
-    geo8 = ["geo8_%d" % i for i in range(4)]
 
-    def codes(f, lst, key):
-        op("v", lambda: V.tensor_copy(T["call%d" % f][:], T["cw%d" % f][:, 0:672].indirect(lst[:, 0:16])),
-           ["cw%d" % f, key], ["call%d" % f])
+    def codes(f, lst, key, q):
+        o, i = T["call%d" % f][:], T["cw%d" % f][:, 0:672].indirect(lst[:, 0:16])
+        op(q, lambda: V.tensor_copy(o, i) if q == "v" else S.activation(o, i, AF.Copy), ["cw%d" % f, key], ["call%d" % f])
 
     def c2(n):
         cl = T["call%d" % (n % 2)]
-        op("p", lambda: mms([[(T.psm[:, O_C2 + 32 * i:O_C2 + 32 * i + 32], (T.dh0, T.dh1)[h][:], cl[:, slot_at(n // 2, i, h):256:8])
-                              for h in (0, 1)] for i in range(4)]), ["call%d" % (n % 2), "dh0", "dh1"], ["c2"], ["m"])
+        op("p", lambda: mms([[(T.psm[:, O_C2 + 32 * s:O_C2 + 32 * s + 32], (T.dh0, T.dh1)[h][:], cl[:, slot_at(n // 2, s, h):256:8])
+                              for h in (0, 1)] for s in range(4)]), ["call%d" % (n % 2), "dh0", "dh1"], ["c2"], ["m"])
+
+    def c2_out(n):
+        op("s", lambda: S.activation(T["c2s%d" % (n % 2)][:], T.psm[:, O_C2:O_C2 + 128], AF.Copy), ["c2"], ["c2s%d" % (n % 2)], ["m"])
 
     def se_list(f):
         cl = T["call%d" % f]
         op("p", lambda: mms([[(T.psm[:, O_SEL:O_SEL + 16], T.bs[:, 15 - q:143 - q], cl[:, q:256:16]) for q in range(16)]]),
            ["call%d" % f, "bs1"], ["selp"], ["m"])
-        op("v", lambda: V.tensor_copy(T["sel%d" % f][:], T.psm[:, O_SEL:O_SEL + 16]), ["selp"], ["sel%d" % f], ["m"])
 
-    codes(0, T.lst0, "lst0")
+    def se_list_out(f):
+        move(SELC_ON, T["sel%d" % f][:], T.psm[:, O_SEL:O_SEL + 16], ["selp"], ["sel%d" % f], ["m"])
+
+    codes(0, T.lst0, "lst0", "s")
     op("v", lambda: V.tensor_scalar(T.neg[:], T.idn[:], -1.0, None, OP.mult), ["idn"], ["neg"])
-    codes(1, T.lst0, "lst0")
-    se_list(0)
-    op("v", lambda: V.tensor_scalar(T.adr0[:], T.i64[:, 0:16], 42.0, T.cols[:, 3:4], OP.mult, OP.add), ["i64", "c3"], ["adr0"])
-    op("v", lambda: V.tensor_scalar(T.hd0[:], T.i64[:, 0:16], 42.0, T.cols[:, 4:5], OP.mult, OP.add), ["i64", "c4"], ["hd0"])
-    se_list(1)
     c2(0)
+    c2_out(0)
+    codes(1, T.lst0, "lst0", "s")
+    op("v", lambda: V.memset(T.rst[:, 0:1024:8], 256.0), ["rst"], ["rst"])
+    op("v", lambda: V.tensor_scalar(T.hd0[:], T.i64[:, 0:16], 42.0, T.cols[:, 4:5], OP.mult, OP.add), ["i64", "c4"], ["hd0"])
+    op("p", lambda: mms([[(T.psq[:, 128 * i + 32 * s:128 * i + 32 * s + 32], T.idn[:], T.glo[:, 32 * i:32 * i + 32])]
+                         for i in range(6) for s in range(4)]), ["glo", "idn"], ["geo"])
+    move("v", T.pew0[:, 2048:4096], T.pew0[:, 0:2048], ["pe0"], ["pew0"])
 
-    def neigh(n, j0, j1):
+    def product(n, j):
         f = n % 2
-        op("s", lambda: S.activation(T.cu[:, 128 * j0:128 * j1],
-                                     T.win[:, 512 * n:512 * n + 512].indirect(T.nbl[:, 24 * f + 8 * j0:24 * f + 8 * j1]), AF.Copy),
-           ["own%d" % n, "far%d" % n, "nbl"], ["cu%d" % j for j in range(j0, j1)])
+        op("v", lambda: V.tensor_tensor(T.y0[:, 128 * j:128 * j + 128],
+                                        T.win[:, 512 * n:512 * n + 512].indirect(T.nbl[:, 3 * f + j, :]),
+                                        T["c2s%d" % f][:], OP.mult), ["own%d" % n, "far%d" % n, "c2s%d" % f] + nbl, ["y0_%d" % j])
 
-    def products(n, j0, j1):
-        for j in range(j0, j1):
-            op("v", lambda: V.tensor_tensor(T.psm[:, O_PR + 128 * j:O_PR + 128 * j + 128], T.cu[:, 128 * j:128 * j + 128],
-                                            T.psm[:, O_C2:O_C2 + 128], OP.mult), ["cu%d" % j, "c2"], ["pr%d" % j], ["m"])
+    def wrapped(n, js):
+        j0, j1 = js[0], js[-1] + 1
+        op("v", lambda: V.tensor_scalar(T.y2[:, 128 * j0:128 * j1], T.y0[:, 128 * j0:128 * j1], 3, 2047, OP.arith_shift_right,
+                                        OP.bitwise_and), ["y0_%d" % j for j in js], ["y2_%d" % j for j in js])
 
-    def shifted(n, j0, j1):
+    def offsets(n, js):
+        f, j0, j1 = n % 2, js[0], js[-1] + 1
+        op("v", lambda: V.tensor_tensor(T["idx%d" % f][:, 128 * j0:128 * j1], T.y2[:, 128 * j0:128 * j1],
+                                        T.psq[:, 384 * f + 128 * j0:384 * f + 128 * j1], OP.add),
+           ["y2_%d" % j for j in js] + ["geo"], ["idx%d_%d" % (f, j) for j in js])
+
+    def picked(n, j, ss):
         f = n % 2
-        op("v", lambda: V.tensor_tensor(T.y1[:, 128 * j0:128 * j1], T.psm[:, O_PR + 128 * j0:O_PR + 128 * j1],
-                                        T.geo8[:, 3 * f + j0:3 * f + j1, :], OP.add),
-           ["pr%d" % j for j in range(j0, j1)] + geo8, ["y1_%d" % j0], ["m"])
+        return T["pew%d" % f][:, 0:4096].indirect(T["idx%d" % f][:, 128 * j + 32 * ss[0]:128 * j + 32 * ss[-1] + 32])
 
-    def wrapped(n, j0, j1):
-        op("v", lambda: V.tensor_scalar(T.y2[:, 128 * j0:128 * j1], T.y1[:, 128 * j0:128 * j1], 3, 2047, OP.arith_shift_right,
-                                        OP.bitwise_and), ["y1_%d" % j0], ["y2_%d" % j0])
+    def blocks(buf, j, ks):
+        return buf[:, 512 * (4 * j + ks[0]):512 * (4 * j + ks[-1] + 1)]
 
-    def offsets(n, j0, j1):
+    def keys(c, n, j, ks):
+        return ["%s%d_%d_%d" % (c, n % 2, j, k) for k in ks]
+
+    plain, where, ring = set(), {}, [0, 1, 2, 3]
+
+    def raw(n, j, ss, q="s"):
         f = n % 2
-        op("v", lambda: V.tensor_copy(T["idx%d" % f][:, 128 * j0:128 * j1], T.y2[:, 128 * j0:128 * j1]), ["y2_%d" % j0],
-           ["idx%d_%d" % (f, j) for j in range(j0, j1)])
+        o, i = blocks(T["ee%d" % f], j, ss), picked(n, j, ss)
+        plain.update((n, j, s) for s in ss)
+        op(q, lambda: V.tensor_copy(o, i) if q == "v" else S.activation(o, i, AF.Copy),
+           ["pew%d" % f, "idx%d_%d" % (f, j)], keys("e", n, j, ss))
 
-    def gather(n, k, q):
+    def fused(n, j, ss):
+        f, ks = n % 2, [s - 2 for s in ss]
+        op("v", lambda: V.tensor_tensor(blocks(T["dd%d" % f], j, ks), picked(n, j, ss), blocks(T["ee%d" % f], j, ks), OP.subtract),
+           ["pew%d" % f, "idx%d_%d" % (f, j)] + keys("e", n, j, ks), keys("f", n, j, ks))
+
+    def diff(n, j, ks):
         f = n % 2
-        x, c = GATHERS[k]
-        src = T["pew%d" % f][:, 0:2048].indirect(T["idx%d" % f][:, 32 * x:32 * (x + c)])
-        out = T["ee%d" % f][:, 512 * x:512 * (x + c)]
-        r, w = ["pew%d" % f, "idx%d_%d" % (f, x // 4)], ["e%d_%d" % (f, y) for y in range(x, x + c)]
-        if q == "v":
-            op("v", lambda: V.tensor_copy(out, src), r, w)
-        else:
-            op("s", lambda: S.activation(out, src, AF.Copy), r, w)
-
-    where = {}
-
-    def diff(n, k):
-        f = n % 2
-        i = ring[0] % 3
-        ring[0] += 1
-        where[n, k] = i
-        d, e = psd[i], T["ee%d" % f]
-        grps, r = [], []
-        x, c = DIFFS[k]
-        for y in range(x, x + c):
-            lo, z = 512 * (y - x), 4 * (y // 4) + (y + 1) % 4
-            r += ["e%d_%d" % (f, y), "e%d_%d" % (f, z)]
-            grp = [(d[:, lo:lo + 512], T.idn[:], e[:, 512 * y:512 * y + 512])]
-            if y % 4 == 0 and n // 2 != 1:
-                grp += [(d[:, lo + q:lo + 512:16], T.neg[:], e[:, 512 * z + (q + 8) % 16:512 * z + 512:16]) for q in range(16)]
+        e, d = T["ee%d" % f], T["dd%d" % f]
+        first = [i for i in ring if i % len(ks) == 0 and all(i + y in ring for y in range(len(ks)))][0]
+        grps, r, bk = [], [], []
+        for y, k in enumerate(ks):
+            i = where[n, j, k] = first + y
+            ring.remove(i)
+            s, z = OWNER[k], RIVAL[OWNER[k]]
+            terms = [(T.idn[:], blocks(e, j, [s]), 0)]
+            r += keys("e", n, j, [s])
+            if (n, j, z) in plain:
+                terms.append((T.neg[:], blocks(e, j, [z]), 1))
+                r += keys("e", n, j, [z])
             else:
-                grp.append((d[:, lo:lo + 512], T.neg[:], e[:, 512 * z:512 * z + 512]))
-            grps.append(grp)
-        op("p", lambda: mms(grps), r + ["idn", "neg"], ["d%d" % i], ["d%d" % i])
+                terms += [(T.neg[:], blocks(e, j, [z - 2]), 1), (T.neg[:], blocks(d, j, [z - 2]), 1)]
+                r += keys("e", n, j, [z - 2]) + keys("f", n, j, [z - 2])
+            o = T.psd[:, 512 * i:512 * i + 512]
+            if k == 3 and n // 2 != 1:
+                grps.append([(o, terms[0][0], terms[0][1])] + [(o[:, q:512:16], w, src[:, q ^ 8:512:16])
+                                                               for w, src, x in terms[1:] for q in range(16)])
+            else:
+                grps.append([(o, w, src) for w, src, x in terms])
+            bk.append("d%d" % i)
+        op("p", lambda: mms(grps), r + ["idn", "neg"], bk, bk)
 
-    def least(n, k):
-        f, i = n % 2, where[n, k]
-        x, c = DIFFS[k]
-        op("v", lambda: V.tensor_tensor_scan(T["mm%d" % f][:, 512 * x:512 * (x + c)], T.rst[:, 0:512 * c], psd[i][:, 0:512 * c], 0.0,
-                                             OP.add, OP.min), ["d%d" % i, "rst"], ["m%d_%d" % (f, y) for y in range(x, x + c)], ["d%d" % i])
+    def banks(n, j, ks):
+        i = where[n, j, ks[0]]
+        ring.extend(range(i, i + len(ks)))
+        return T.psd[:, 512 * i:512 * (i + len(ks))], ["d%d" % (i + y) for y in range(len(ks))]
+
+    def evac(n, j, ks):
+        src, bk = banks(n, j, ks)
+        op("s", lambda: S.activation(blocks(T["dd%d" % (n % 2)], j, ks), src, AF.Copy), bk, keys("f", n, j, ks), bk)
+
+    def least(n, j, ks, direct=False):
+        f = n % 2
+        src, r, bk = blocks(T["dd%d" % f], j, ks), keys("f", n, j, ks), []
+        if direct:
+            src, bk = banks(n, j, ks)
+            r = bk
+        op("v", lambda: V.tensor_tensor_scan(blocks(T["mm%d" % f], j, ks), T.rst[:, 0:512 * len(ks)], src, 0.0, OP.add, OP.min),
+           r + ["rst"], keys("m", n, j, ks), bk)
 
     def selfs(n):
         f = n % 2
-        op("v", lambda: V.tensor_copy(T["sev%d" % f][:], T["sew%d" % f][:, 0:2048].indirect(T["sel%d" % f][:, 0:16])),
-           ["sew%d" % f, "sel%d" % f], ["sev%d" % f])
+        move(SELF_ON, T["sev%d" % f][:], T["sew%d" % f][:, 0:2048].indirect(T["sel%d" % f][:, 0:16]),
+             ["sew%d" % f, "sel%d" % f], ["sev%d" % f])
 
     G = T.psg
-    places = [(i, h) for i in range(4) for h in (0, 1)]
+    places = [(k, h) for k in range(4) for h in (0, 1)]
 
     def sums(n, j):
-        m = T["mm%d" % (n % 2)]
-        if n < 4:
-            return [(G[:, 0:256], T.idn[:], m[:, 2048 * j + 7:2048 * j + 2048:8])]
-        return [(G[:, slot_at(2, i, h):256:8], T.idn[:], m[:, 2048 * j + 512 * i + 8 * h + 7:2048 * j + 512 * i + 512:16]) for i, h in places]
-
-    def gap_first(n):
         f, t = n % 2, n // 2
-        v = T["sev%d" % f]
-        if n < 4:
-            grp = sums(n, 0)
-            for i, h in places:
-                a, o = slot_at(t, i, h), G[:, 64 * i + h:64 * i + 64:2]
-                grp += [(o, T.idn[:], v[:, a:256:8]), (o, T.neg[:], v[:, (a + t + 1) % 8:256:8])]
+        m, v = T["mm%d" % f][:, 2048 * j + 7:2048 * j + 2048:8], T["sev%d" % f]
+        if t < 2:
+            grp = [(G[:, 0:256], T.idn[:], m)]
         else:
-            grp = [(G[:, 0:256], T.idn[:], v[:])] + [(G[:, a:256:8], T.neg[:], v[:, (a + 3) % 8:256:8]) for a in range(8)] + sums(n, 0)
-        op("p", lambda: mms([grp + sums(n, 1)], stop=False), ["sev%d" % f, "idn", "neg"] + ["m%d_%d" % (f, y) for y in range(8)], ["gap"], ["g"])
+            grp = [(G[:, slot_at(t, OWNER[k], h):256:8], T.idn[:], m[:, slice(*gap_cols(t, k, h, 0, 1))]) for k, h in places]
+        r = keys("m", n, j, range(4)) + ["idn"]
+        if j == 0:
+            r += ["sev%d" % f, "neg"]
+            if t < 2:
+                for k, h in places:
+                    a, o = slot_at(t, OWNER[k], h), G[:, slice(*gap_cols(t, k, h, 0, 1))]
+                    grp += [(o, T.idn[:], v[:, a:256:8]), (o, T.neg[:], v[:, (a + t + 1) % 8:256:8])]
+            else:
+                grp = [(G[:, 0:256], T.idn[:], v[:])] + [(G[:, a:256:8], T.neg[:], v[:, (a + 3) % 8:256:8]) for a in range(8)] + grp
+        op("p", lambda: mms([grp], start=j == 0, stop=j == 2), r, ["gap"], ["g"])
 
-    def gap_last(n):
-        op("p", lambda: mms([sums(n, 2)], start=False), ["m%d_%d" % (n % 2, y) for y in range(8, 12)], ["gap"], ["g"])
+    def signs(n):
+        op("s", lambda: S.activation(T.ind[:], G[:, 0:256], AF.Sign, bias=-0.5), ["gap"], ["ind"], ["g"])
 
     def count(n):
-        at = {slot_at(n // 2, i, h): 64 * i + h for i, h in places}
-        op("v", lambda: V.tensor_scalar(T.ind[:], G[:, 0:256], 0.5, None, OP.is_gt), ["gap"], ["ind"], ["g"])
+        t = n // 2
+        at = {slot_at(t, OWNER[k], h): (k, h) for k, h in places}
         op("p", lambda: mms([[(T.psm[:, O_CNT:O_CNT + 16], T.bc[:, 15 - q:143 - q],
-                               T.ind[:, at[q % 8] + 2 * (q // 8):at[q % 8] - at[q % 8] % 64 + 64:4]) for q in range(16)]]),
+                               T.ind[:, slice(*gap_cols(t, at[q % 8][0], at[q % 8][1], q // 8, 2))]) for q in range(16)]]),
            ["ind", "bc1"], ["cnt"], ["m"])
 
     def deaths(n):
+        if DEAD_ON == "v":
+            op("v", lambda: V.tensor_scalar(T.dead[:], T.psm[:, O_CNT:O_CNT + 16], 15.5, None, OP.is_gt), ["cnt"], ["dead"], ["m"])
+        else:
+            op("s", lambda: S.activation(T.dead[:], T.psm[:, O_CNT:O_CNT + 16], AF.Relu, bias=-15.0), ["cnt"], ["dead"], ["m"])
+
+    def prefix(n):
         f = n % 2
         hd, key = (T.hd0, "hd0") if n < 2 else (T["hd%d" % (f + 1)], "hd%d" % (f + 1))
-        op("v", lambda: V.tensor_scalar(T.dead[:], T.psm[:, O_CNT:O_CNT + 16], 15.5, None, OP.is_gt), ["cnt"], ["dead"], ["m"])
         op("p", lambda: mms([[(T.psm[:, O_PRE:O_PRE + 16], T.idn[:], hd[:]), (T.psm[:, O_PRE:O_PRE + 16], T.ltri[:], T.dead[:])]]),
            ["dead", "ltri", key], ["pre"], ["m"])
 
     def refill(n):
         f = n % 2
-        ad, key = T["adr%d" % (f + 1)], "adr%d" % (f + 1)
-        old, okey = (T.adr0, "adr0") if n < 2 else (ad, key)
-        op("v", lambda: V.tensor_tensor(ad[:], T.psm[:, O_PRE:O_PRE + 16], old[:], OP.max), ["pre", okey], [key], ["m"])
-        op("v", lambda: V.tensor_copy(T.lst[:], ad[:]), [key], ["lst"])
-        codes(f, T.lst, "lst")
+        key = "lst%d" % (f + 1)
+        old = "lst0" if n < 2 else key
+        op("v", lambda: V.tensor_tensor(T[key][:], T.psm[:, O_PRE:O_PRE + 16], T[old][:], OP.max), ["pre", old], [key], ["m"])
+
+    def outgoing(n):
+        f = n % 2
         cl = T["call%d" % f]
         op("p", lambda: mms([[(T.psm[:, O_L1 + 32 * b:O_L1 + 32 * b + 32], T.zz[:, 136 * b + 7 - u:136 * b + 135 - u],
                                cl[:, u:256:8]) for u in range(8)] for b in (0, 1)]),
            ["call%d" % f, "zz0", "zz1"], ["l1"], ["m"])
 
     def heads(n):
-        f = n % 2
         o = T.psm[:, O_HD:O_HD + 16]
-        op("p", lambda: mms([[(o, T.one8[:], T.dead[:]), (o, T.idn[:], T.hd0[:])]]), ["dead", "one8", "hd0"], ["hdp"], ["m"])
-        op("v", lambda: V.tensor_copy(T["hd%d" % (f + 1)][:], o), ["hdp"], ["hd%d" % (f + 1)], ["m"])
+        if n < 2:
+            op("p", lambda: mms([[(o, T.one8[:], T.dead[:]), (o, T.idn[:], T.hd0[:])]]), ["dead", "one8", "hd0"], ["hdp"], ["m"])
+
+    def heads_out(n):
+        if n < 2:
+            op("s", lambda: S.activation(T["hd%d" % (n + 1)][:], T.psm[:, O_HD:O_HD + 16], AF.Copy), ["hdp"], ["hd%d" % (n + 1)], ["m"])
 
     def alive(n):
         op("v", lambda: V.tensor_scalar(T.ind[:], G[:, 0:256], 0.5, 2.0 ** -16, OP.is_lt, OP.subtract), ["gap"], ["ind"], ["g"])
+
+    def living(n):
         op("p", lambda: g.tensor.matmul(T.psm[:, 0:256], T.o16[:], T.ind[:], True, True), ["ind", "o16"], ["liv"], ["m"])
 
-    def results(n):
+    def gaps_out(n):
         f = n % 2
-        yg, yc = T["ygs%d" % f], T["ycs%d" % f]
-        qs = "yy" if n == 4 else "ys"
-        op("v", lambda: V.tensor_copy(yg[:], G[:, 0:256]), ["gap"], ["ygs%d" % f], ["g"])
-        dmas("dog%d" % f, [(qs[b], T.yg[64 * f:64 * f + 64, 256 * b:256 * b + 256], yg[64 * b:64 * b + 64, :]) for b in (0, 1)],
+        yg = T["ygs%d" % f]
+        op("s", lambda: S.activation(yg[:], G[:, 0:256], AF.Copy), ["gap"], ["ygs%d" % f], ["g"])
+        dmas("dog%d" % f, [("ys"[b * f], T.yg[64 * f:64 * f + 64, 256 * b:256 * b + 256], yg[64 * b:64 * b + 64, :]) for b in (0, 1)],
              reads=["ygs%d" % f])
+
+    def codes_out(n):
+        f = n % 2
+        yc = T["ycs%d" % f]
         op("v", lambda: V.tensor_tensor(yc[:], T.psm[:, 0:256], T["call%d" % f][:], OP.min), ["liv", "call%d" % f], ["ycs%d" % f], ["m"])
-        dmas("doc%d" % f, [(qs[b], T.yc[4 * f:4 * f + 4, 256 * b:256 * b + 256], yc[64 * b:64 * b + 64:16, :]) for b in (0, 1)],
+        dmas("doc%d" % f, [("y", T.yc[4 * f:4 * f + 4, 256 * b:256 * b + 256], yc[64 * b:64 * b + 64:16, :]) for b in (0, 1)],
              reads=["ycs%d" % f])
 
-    neigh(0, 0, 1)
-    neigh(0, 1, 3)
-    for step in (products, shifted, wrapped, offsets):
-        step(0, 0, 1)
-    products(0, 1, 3)
-    for n in range(6):
-        p = n - 1
-        steps = {"gapl": lambda: gap_last(p), "cnt": lambda: count(p), "dead": lambda: deaths(p), "fill": lambda: refill(p),
-                 "l1": lambda: l1_out(n + 1), "sel": lambda: se_list(p % 2), "head": lambda: heads(p) if p < 2 else None,
-                 "c2": lambda: c2(n + 1), "self": lambda: selfs(n), "gapf": lambda: gap_first(n),
-                 "cu0": lambda: neigh(n + 1, 0, 1), "cu1": lambda: neigh(n + 1, 1, 3),
-                 "p0": lambda: products(n + 1, 0, 1), "x0": lambda: shifted(n + 1, 0, 1), "y0": lambda: wrapped(n + 1, 0, 1),
-                 "z0": lambda: offsets(n + 1, 0, 1), "p1": lambda: products(n + 1, 1, 3), "x1": lambda: shifted(n, 1, 3),
-                 "y1": lambda: wrapped(n, 1, 3), "z1": lambda: offsets(n, 1, 3),
-                 "alive": lambda: alive(p), "res": lambda: results(p)}
-        for w in ORDER.get(n, ORDER[1]).split():
-            if w in steps:
-                steps[w]()
-            elif w[0] == "g":
-                gather(n, int(w[1:]), "s")
-            elif w[0] == "G":
-                gather(n, int(w[1:]), "v")
-            elif w[0] == "d":
-                diff(n, int(w[1:]))
+    named = {"ind": signs, "cnt": count, "dead": deaths, "pre": prefix, "fill": refill,
+             "call": lambda n: codes(n % 2, T["lst%d" % (n % 2 + 1)], "lst%d" % (n % 2 + 1), CALL_ON), "out": outgoing, "l1": lambda n: l1_out(n + 2, "s"),
+             "sel": lambda n: se_list(n % 2), "selc": lambda n: se_list_out(n % 2), "head": heads, "headc": heads_out,
+             "c2": c2, "c2c": c2_out, "self": selfs, "alive": alive, "liv": living, "yg": gaps_out, "yc": codes_out}
+    by_j = {"s": sums, "p": product}
+    by_js = {"y": wrapped, "z": offsets}
+    by_block = {"r": raw, "R": lambda n, j, ss: raw(n, j, ss, "v"), "f": fused, "d": diff, "e": evac, "m": least,
+                "P": lambda n, j, ks: least(n, j, ks, True)}
+    only = {"c2": range(1, 6), "c2c": range(1, 6), "self": range(6), "sel": range(6), "selc": range(6), "head": range(2), "headc": range(2)}
+    only.update({w: range(4, 6) for w in ("alive", "liv", "yg", "yc")})
+    for n in range(-2, 8):
+        for w in ORDER.get(n, ORDER.get("all", "")).split():
+            m = n + w.count("+") - w.count("-")
+            w = w.rstrip("+-")
+            if m not in (only.get(w, range(4)) if w in named else range(6)):
+                continue
+            if w in named:
+                named[w](m)
+            elif w[0] in by_j:
+                by_j[w[0]](m, int(w[1:]))
+            elif w[0] in by_js:
+                by_js[w[0]](m, [int(c) for c in w[1:]])
             else:
-                least(n, int(w[1:]))
-    gap_last(5)
-    alive(5)
-    results(5)
+                by_block[w[0]](m, int(w[1]), [int(c) for c in w[2:]])
 
     for sem in total:
         if max(seen[q].get(sem, 0) for q in Q) < total[sem]:

from concourse.bass import DstId, RemoteDMATransfer
from concourse.mybir import AluOpType as OP, ActivationFunctionType as AF

CD = "float16"
BF, F32, I32, U16 = "bfloat16", "float32", "int32", "uint16"

SCRATCH = {}
for _dt, _bufs in (
        (I32, {"candi": [32, 21], "nbi": [12, 4], "nbs": [12, 2], "ghl": [24], "i64": [64], "pcol": [4], "ah": [4],
               "y0": [384], "y2": [384], "sew0": [2048], "sew1": [2048]}),
        (CD, {"candf": [672], "cand8": [32, 8], "hd0": [16], "hd1": [16], "hd2": [16], "call0": [256], "call1": [256],
              "sev0": [256], "sev1": [256], "glo": [192]}),
        (U16, {"nbl": [6, 8], "ghu": [24], "lst0": [16], "lst1": [16], "lst2": [16], "sel0": [16], "sel1": [16], "idx0": [384],
               "idx1": [384]}),
        (F32, {"ghi": [192], "cols": [8], "win": [3072], "c2s0": [128], "c2s1": [128], "cw0": [672], "cw1": [672],
               "ygs0": [256], "ygs1": [256], "ycs0": [256], "ycs1": [256]}),
        (BF, {"ones": [128], "big": [128], "z0": [544], "r0": [256], "zz": [272], "bc": [144], "bs": [144], "idn": [128],
              "neg": [128], "dh0": [128], "dh1": [128], "one8": [128], "ltri": [128], "o16": [128], "rst": [1024], "ind": [256],
              "dead": [16], "pew0": [4096], "pew1": [4096], "ee0": [6144], "ee1": [6144], "dd0": [6144],
              "dd1": [6144], "mm0": [6144], "mm1": [6144]})):
    for _k in _bufs:
        SCRATCH[_k] = ("sbuf", [128] + _bufs[_k], _dt)
for _k, _n in (("psd", 2048), ("psq", 1024), ("psg", 512), ("psm", 512)):
    SCRATCH[_k] = ("psum", [128, _n], F32)

SEMAPHORES = (["cv", "cs", "cp", "cg", "dcand", "dtab", "dpe0", "dpe1", "dse0", "dse1", "dog0", "dog1", "doc0", "doc1"]
              + ["arr%d" % n for n in range(6)] + ["snt%d" % n for n in range(6)])

O_C2, O_L1, O_CNT, O_PRE, O_HD, O_SEL = 256, 384, 448, 464, 480, 496
PLACE = [2, 0, 1, 3]
OWNER = [2, 3, 0, 1]
RIVAL = [3, 2, 0, 1]
DEAD_ON, SELF_ON, SELC_ON, CALL_ON = "v", "v", "v", "s"
ORDER = {
    "all": "pre- fill- d03 alive- call- r20 f03 out- f13 l1- r22 f12 d02 d12 c2+ d20 e03 self e02 c2c+ d13 r23 head- m101 d22 m001 "
           "m023 P20 r21 d21 e12 liv- p0+ p2+ e13 d23 y0+ p1+ z0+ yg- P22 headc- P21 m123 P23 s0 r001+ sel+ s1 s2 y12+ selc+ ind "
           "z12+ f02+ r11+ r10+ cnt yc- dead",
}


def slot_at(t, s, h):
    i, step = PLACE[s], t + 1
    if step % 2 == 0:
        return 2 * i + h
    return (step * ((i + 3) % 4 + 4 * h)) % 8


def gap_cols(t, k, h, x0, dx):
    return 64 * k + h + 2 * x0, 64 * k + 64, 2 * dx


def rank_program(g, core, T, topo):
    rank = T.rank_of(core)
    if rank is None:
        return
    Q = {"v": g.vector, "s": g.scalar, "p": g.tensor, "g": g, "y": g.sync}
    own = {"v": "cv", "s": "cs", "p": "cp", "g": "cg"}
    total = {}
    seen = {q: {} for q in Q}
    wr, rd, bank = {}, {}, {}

    def need(q, tok):
        sem, val = tok[0], tok[1]
        if seen[q].get(sem, 0) < val:
            Q[q].wait_ge(T.sem[sem], val)
            seen[q][sem] = val

    def deps(q, reads, writes, banks):
        want = {}
        toks = [wr[k] for k in reads]
        for k in writes:
            toks += ([wr[k]] if k in wr else []) + rd.get(k, [])
        toks = [t for t in toks if not (q == "p" and t[2] == "p")]
        toks += [bank[k] for k in banks if k in bank and bank[k][2] != q]
        for t in toks:
            want[t[0]] = max(want.get(t[0], 0), t[1])
        for sem in want:
            need(q, (sem, want[sem]))

    def note(tok, reads, writes, banks):
        for k in reads:
            rd.setdefault(k, []).append(tok)
        for k in writes:
            wr[k] = tok
            rd[k] = []
        for k in banks:
            bank[k] = tok

    def op(q, fn, reads=(), writes=(), banks=()):
        deps(q, reads, writes, banks)
        sem = own[q]
        total[sem] = total.get(sem, 0) + 1
        fn().then_inc(T.sem[sem], 1)
        note((sem, total[sem], q), reads, writes, banks)

    def dmas(sem, items, reads=(), writes=()):
        for q, o, i in items:
            deps(q, reads, writes, ())
            Q[q].dma_start(o, i).then_inc(T.sem[sem], 16)
        total[sem] = total.get(sem, 0) + 16 * len(items)
        note((sem, total[sem], "dma"), reads, writes, ())

    def mms(items, start=True, stop=True):
        last = None
        for grp in items:
            for i, (o, l, r) in enumerate(grp):
                last = g.tensor.matmul(o, l, r, start and i == 0, stop and i == len(grp) - 1)
        return last

    def select(out, src, pattern, cmp, fill, base, step, reads, writes):
        op("g", lambda: g.affine_select(out, src, pattern, cmp, fill, base, step), reads, writes)

    V, S = g.vector, g.scalar

    def move(q, o, i, reads, writes, banks=()):
        op(q, lambda: V.tensor_copy(o, i) if q == "v" else S.activation(o, i, AF.Copy), reads, writes, banks)

    others = [c for c in T.cores if c != core]
    near = [c for c in others if c in topo.cores_of(core)]
    far = [c for c in others if c not in near]

    def engines_for(src):
        o = [c for c in T.cores if c != src]
        nr = [c for c in o if c in topo.cores_of(src)]
        fr = [c for c in o if c not in nr]
        fe = [e for e in topo.engines(src, fr[0]) if all(e in topo.engines(src, c) for c in fr)]
        ne = [e for e in topo.engines(src, nr[0]) if e not in fe][0:4:2]
        return fe, ne

    def arrivals():
        n = 0
        for c in others:
            fe, ne = engines_for(c)
            n += len(ne) if c in near else len(fe)
        return n

    def send(n):
        piece = T.win[:, 512 * n + 64 * rank:512 * n + 64 * rank + 64]
        deps("g", ["own%d" % n], [], ())
        fe, ne = engines_for(core)
        trs = []
        for dsts, es in ((far, fe), (near, ne)):
            ids = []
            for c in dsts:
                rid, pid = topo.addr(c, core)
                ids.append(DstId(rid=rid, pnc=pid))
            trs.append(RemoteDMATransfer(dst_ids=ids, dma_engine_mask=sum(1 << e for e in es), remote_sem=T.sem["arr%d" % n],
                                         srcs=[piece], dsts=[piece] * len(dsts)))
        g.remote_dma_fused(trs, local_sem=T.sem["snt%d" % n])
        total["snt%d" % n] = len(fe) + len(ne)
        total["arr%d" % n] = arrivals()
        wr["far%d" % n] = ("arr%d" % n, total["arr%d" % n], "dma")
        wr["sent%d" % n] = ("snt%d" % n, total["snt%d" % n], "dma")

    dmas("dcand", [("y", T.candi[0:16, :, :], T.cand[:])], writes=["candi"])
    dmas("dtab", [("ys"[t], T.nbi[64 * b:64 * b + 64, 6 * t + 3 * f:6 * t + 3 * f + 3, :], (T.nb, T.geo)[t][64 * f:64 * f + 64, :])
                  for t in (0, 1) for f in (0, 1) for b in (0, 1)], writes=["nbi"])
    dmas("dpe0", [("ys"[b], T.pew0[64 * b:64 * b + 64, 0:2048], T.pe[0:64, :]) for b in (0, 1)], writes=["pe0"])

    op("v", lambda: V.memset(T.ones[:], 1.0), writes=["ones"])
    op("v", lambda: V.memset(T.z0[0:32, :], 0.0), writes=["z0"])
    op("v", lambda: V.memset(T.bs[:], 0.0), writes=["bs"])
    op("g", lambda: g.iota(T.pcol[:, 0:1], [[0, 1]], 0, 1), writes=["pcol"])
    op("g", lambda: g.iota(T.i64[:], [[1, 64]], 0, 0), writes=["i64"])
    for i in range(4):
        select(T.z0[0:16, 136 * i + 7:136 * i + 135:8], T.ones[0:16, 0:16], [[0, 2], [-2, 4], [0, 2]], OP.is_equal, 0.0,
               -(8 * (i // 2) + i % 2), 1, ["ones", "z0"], ["z0_%d" % i])
    select(T.idn[:], T.ones[:], [[-1, 128]], OP.is_equal, 0.0, 0, 1, ["ones"], ["idn"])
    for f in (0, 1):
        select(T.r0[0:16, 128 * f:128 * f + 128], T.ones[0:16, :], [[-1, 2], [-2, 4], [0, 16]], OP.is_equal, 0.0, -8 * f, 1,
               ["ones"], ["r0_%d" % f])
    select(T.bs[:, 15:143:16], T.ones[:, 0:8], [[-16, 8]], OP.is_equal, 0.0, 0, 1, ["ones", "bs"], ["bs1"])
    op("v", lambda: V.memset(T.zz[:], 0.0), writes=["zz"])
    op("v", lambda: V.memset(T.bc[:], 0.0), writes=["bc"])
    op("v", lambda: V.memset(T.big[:], 4096.0), writes=["big"])
    op("v", lambda: V.tensor_scalar(T.ah[:, 0:1], T.pcol[:, 0:1], 7, None, OP.bitwise_and), ["pcol"], ["ah0"])
    op("v", lambda: V.tensor_scalar(T.ah[:, 1:2], T.pcol[:, 0:1], 3, 1, OP.arith_shift_right, OP.bitwise_and), ["pcol"], ["ah1"])
    op("v", lambda: V.memset(T.rst[:], 0.0), writes=["rst"])
    op("v", lambda: V.tensor_copy(T.cols[:, 0:2], T.ah[:, 0:2]), ["ah0", "ah1"], ["c01"])

    op("v", lambda: V.tensor_copy(T.cand8[0:16, :, :], T.candi[0:16, :, 0:8]), ["candi"], ["cand8"])

    def first_l1(f):
        op("p", lambda: mms([[(T.psm[:, O_L1 + 32 * b:O_L1 + 32 * b + 32],
                               T.z0[0:16, 136 * (2 * f + b) + 7 - u:136 * (2 * f + b) + 135 - u], T.cand8[0:16, :, u])
                              for u in range(8)] for b in (0, 1)]),
           ["cand8", "z0_%d" % (2 * f), "z0_%d" % (2 * f + 1)], ["l1"], ["m"])

    def l1_out(n, q):
        o, i = T.win[:, 512 * n + 64 * rank:512 * n + 64 * rank + 64], T.psm[:, O_L1:O_L1 + 64]
        op(q, lambda: V.tensor_copy(o, i) if q == "v" else S.activation(o, i, AF.Copy), ["l1"], ["own%d" % n], ["m"])
        send(n)

    move("s", T.candf[0:16, :], T.candi[0:16, :, :], ["candi"], ["candf"])
    first_l1(0)
    op("v", lambda: V.tensor_scalar(T.cols[:, 2:3], T.cols[:, 1:2], -1.0, 1.0, OP.mult, OP.add), ["c01"], ["c2c"])
    op("v", lambda: V.tensor_scalar(T.cols[:, 3:4], T.cols[:, 1:2], 21.0, T.cols[:, 0:1], OP.mult, OP.add), ["c01"], ["c3"])
    op("v", lambda: V.tensor_scalar(T.cols[:, 4:5], T.cols[:, 1:2], 21.0, 8.0 - 1024.0, OP.mult, OP.add), ["c01"], ["c4"])
    l1_out(0, "s")
    first_l1(1)
    l1_out(1, "s")

    def queue_window(f):
        d = T.psd[:, 1024 * f:1024 * f + 672]
        bk = ["d%d" % (2 * f), "d%d" % (2 * f + 1)]
        op("p", lambda: mms([[(d[:, 0:512], T.r0[0:16, 128 * f:128 * f + 128], T.candf[0:16, 0:512])],
                             [(d[:, 512:672], T.r0[0:16, 128 * f:128 * f + 128], T.candf[0:16, 512:672])]]),
           ["candf", "r0_%d" % f], bk, bk)
        op("s", lambda: S.activation(T["cw%d" % f][:], d, AF.Copy), bk, ["cw%d" % f], bk)

    queue_window(0)
    queue_window(1)

    deps("y", ["sent0"], [], ())
    dmas("dse0", [("y", T.sew0[64 * b:64 * b + 64, :], T.se[0:64, :]) for b in (0, 1)], writes=["sew0"])
    dmas("dpe1", [("y", T.pew1[64 * b:64 * b + 64, 2048 * i:2048 * i + 2048], T.pe[64:128, :]) for b in (0, 1) for i in (0, 1)],
         writes=["pew1"])
    dmas("dse1", [("y", T.sew1[64 * b:64 * b + 64, :], T.se[64:128, :]) for b in (0, 1)], writes=["sew1"])

    for b in (0, 1):
        select(T.zz[:, 136 * b + 7:136 * b + 135:8], T.ones[:, 0:16], [[0, 2], [-16, 4], [0, 2]], OP.is_equal, 0.0, -64 * b, 1,
               ["ones", "zz"], ["zz%d" % b])
    select(T.bc[:, 15:143:16], T.ones[:, 0:8], [[-16, 8]], OP.is_ge, 0.0, 0, 1, ["ones", "bc"], ["bc1"])
    select(T.bc[:, 15:143:16], T.bc[:, 15:143:16], [[16, 8]], OP.is_ge, 0.0, 15, -1, ["bc1"], ["bc1"])
    select(T.one8[:], T.ones[:], [[-8, 16], [0, 8]], OP.is_ge, 0.0, 0, 1, ["ones"], ["one8"])
    select(T.one8[:], T.one8[:], [[8, 16], [0, 8]], OP.is_ge, 0.0, 7, -1, ["one8"], ["one8"])
    select(T.ltri[:], T.one8[:], [[1, 128]], OP.is_gt, 0.0, 0, -1, ["one8"], ["ltri"])
    select(T.ltri[:], T.ltri[:], [[1, 128]], OP.not_equal, 1024.0, 0, -1, ["ltri"], ["ltri"])
    select(T.o16[:], T.big[:], [[-16, 8], [0, 16]], OP.is_ge, 0.0, 0, 1, ["big"], ["o16"])
    select(T.o16[:], T.o16[:], [[16, 8], [0, 16]], OP.is_ge, 0.0, 15, -1, ["o16"], ["o16"])

    for b in (0, 1):
        op("v", lambda: V.tensor_copy(T.nbs[64 * b:64 * b + 64, :, :], T.nbi[64 * b:64 * b + 64, :, 2 * b:2 * b + 2]), ["nbi"], ["nbs%d" % b])
    nbs = ["nbs0", "nbs1"]
    op("v", lambda: V.tensor_scalar(T.lst0[:], T.i64[:, 0:16], 42.0, T.cols[:, 3:4], OP.mult, OP.add), ["i64", "c3"], ["lst0"])
    op("v", lambda: V.tensor_scalar(T.ghl[:, 0:12], T.nbs[:, 6:12, :], 6, None, OP.arith_shift_right), nbs, ["gh"])
    op("v", lambda: V.tensor_scalar(T.ghl[:, 12:24], T.nbs[:, 6:12, :], 63, None, OP.bitwise_and), nbs, ["gl"])
    op("v", lambda: V.tensor_scalar(T.dh0[:], T.idn[:], T.cols[:, 2:3], None, OP.mult), ["idn", "c2c"], ["dh0"])
    op("v", lambda: V.tensor_copy(T.ghu[:], T.ghl[:]), ["gh", "gl"], ["ghu"])
    op("v", lambda: V.tensor_scalar(T.dh1[:], T.idn[:], T.cols[:, 1:2], None, OP.mult), ["idn", "c01"], ["dh1"])
    op("v", lambda: V.tensor_scalar(T.ghi[:], T.i64[:, 0:64].indirect(T.ghu[:, 0:12]), 64.0, None, OP.mult), ["i64", "ghu"], ["ghi"])
    for i in range(4):
        op("v", lambda: V.tensor_copy(T.nbl[:, :, 2 * i:2 * i + 2], T.nbs[:, 0:6, :]), nbs, ["nbl%d" % i])
    nbl = ["nbl%d" % i for i in range(4)]
    op("v", lambda: V.tensor_tensor(T.glo[:], T.i64[:, 0:64].indirect(T.ghu[:, 12:24]), T.ghi[:], OP.add), ["i64", "ghu", "ghi"], ["glo"])

    def codes(f, lst, key, q):
        o, i = T["call%d" % f][:], T["cw%d" % f][:, 0:672].indirect(lst[:, 0:16])
        op(q, lambda: V.tensor_copy(o, i) if q == "v" else S.activation(o, i, AF.Copy), ["cw%d" % f, key], ["call%d" % f])

    def c2(n):
        cl = T["call%d" % (n % 2)]
        op("p", lambda: mms([[(T.psm[:, O_C2 + 32 * s:O_C2 + 32 * s + 32], (T.dh0, T.dh1)[h][:], cl[:, slot_at(n // 2, s, h):256:8])
                              for h in (0, 1)] for s in range(4)]), ["call%d" % (n % 2), "dh0", "dh1"], ["c2"], ["m"])

    def c2_out(n):
        op("s", lambda: S.activation(T["c2s%d" % (n % 2)][:], T.psm[:, O_C2:O_C2 + 128], AF.Copy), ["c2"], ["c2s%d" % (n % 2)], ["m"])

    def se_list(f):
        cl = T["call%d" % f]
        op("p", lambda: mms([[(T.psm[:, O_SEL:O_SEL + 16], T.bs[:, 15 - q:143 - q], cl[:, q:256:16]) for q in range(16)]]),
           ["call%d" % f, "bs1"], ["selp"], ["m"])

    def se_list_out(f):
        move(SELC_ON, T["sel%d" % f][:], T.psm[:, O_SEL:O_SEL + 16], ["selp"], ["sel%d" % f], ["m"])

    codes(0, T.lst0, "lst0", "s")
    op("v", lambda: V.tensor_scalar(T.neg[:], T.idn[:], -1.0, None, OP.mult), ["idn"], ["neg"])
    c2(0)
    c2_out(0)
    codes(1, T.lst0, "lst0", "s")
    op("v", lambda: V.memset(T.rst[:, 0:1024:8], 256.0), ["rst"], ["rst"])
    op("v", lambda: V.tensor_scalar(T.hd0[:], T.i64[:, 0:16], 42.0, T.cols[:, 4:5], OP.mult, OP.add), ["i64", "c4"], ["hd0"])
    op("p", lambda: mms([[(T.psq[:, 128 * i + 32 * s:128 * i + 32 * s + 32], T.idn[:], T.glo[:, 32 * i:32 * i + 32])]
                         for i in range(6) for s in range(4)]), ["glo", "idn"], ["geo"])
    move("v", T.pew0[:, 2048:4096], T.pew0[:, 0:2048], ["pe0"], ["pew0"])

    def product(n, j):
        f = n % 2
        op("v", lambda: V.tensor_tensor(T.y0[:, 128 * j:128 * j + 128],
                                        T.win[:, 512 * n:512 * n + 512].indirect(T.nbl[:, 3 * f + j, :]),
                                        T["c2s%d" % f][:], OP.mult), ["own%d" % n, "far%d" % n, "c2s%d" % f] + nbl, ["y0_%d" % j])

    def wrapped(n, js):
        j0, j1 = js[0], js[-1] + 1
        op("v", lambda: V.tensor_scalar(T.y2[:, 128 * j0:128 * j1], T.y0[:, 128 * j0:128 * j1], 3, 2047, OP.arith_shift_right,
                                        OP.bitwise_and), ["y0_%d" % j for j in js], ["y2_%d" % j for j in js])

    def offsets(n, js):
        f, j0, j1 = n % 2, js[0], js[-1] + 1
        op("v", lambda: V.tensor_tensor(T["idx%d" % f][:, 128 * j0:128 * j1], T.y2[:, 128 * j0:128 * j1],
                                        T.psq[:, 384 * f + 128 * j0:384 * f + 128 * j1], OP.add),
           ["y2_%d" % j for j in js] + ["geo"], ["idx%d_%d" % (f, j) for j in js])

    def picked(n, j, ss):
        f = n % 2
        return T["pew%d" % f][:, 0:4096].indirect(T["idx%d" % f][:, 128 * j + 32 * ss[0]:128 * j + 32 * ss[-1] + 32])

    def blocks(buf, j, ks):
        return buf[:, 512 * (4 * j + ks[0]):512 * (4 * j + ks[-1] + 1)]

    def keys(c, n, j, ks):
        return ["%s%d_%d_%d" % (c, n % 2, j, k) for k in ks]

    plain, where, ring = set(), {}, [0, 1, 2, 3]

    def raw(n, j, ss, q="s"):
        f = n % 2
        o, i = blocks(T["ee%d" % f], j, ss), picked(n, j, ss)
        plain.update((n, j, s) for s in ss)
        op(q, lambda: V.tensor_copy(o, i) if q == "v" else S.activation(o, i, AF.Copy),
           ["pew%d" % f, "idx%d_%d" % (f, j)], keys("e", n, j, ss))

    def fused(n, j, ss):
        f, ks = n % 2, [s - 2 for s in ss]
        op("v", lambda: V.tensor_tensor(blocks(T["dd%d" % f], j, ks), picked(n, j, ss), blocks(T["ee%d" % f], j, ks), OP.subtract),
           ["pew%d" % f, "idx%d_%d" % (f, j)] + keys("e", n, j, ks), keys("f", n, j, ks))

    def diff(n, j, ks):
        f = n % 2
        e, d = T["ee%d" % f], T["dd%d" % f]
        first = [i for i in ring if i % len(ks) == 0 and all(i + y in ring for y in range(len(ks)))][0]
        grps, r, bk = [], [], []
        for y, k in enumerate(ks):
            i = where[n, j, k] = first + y
            ring.remove(i)
            s, z = OWNER[k], RIVAL[OWNER[k]]
            terms = [(T.idn[:], blocks(e, j, [s]), 0)]
            r += keys("e", n, j, [s])
            if (n, j, z) in plain:
                terms.append((T.neg[:], blocks(e, j, [z]), 1))
                r += keys("e", n, j, [z])
            else:
                terms += [(T.neg[:], blocks(e, j, [z - 2]), 1), (T.neg[:], blocks(d, j, [z - 2]), 1)]
                r += keys("e", n, j, [z - 2]) + keys("f", n, j, [z - 2])
            o = T.psd[:, 512 * i:512 * i + 512]
            if k == 3 and n // 2 != 1:
                grps.append([(o, terms[0][0], terms[0][1])] + [(o[:, q:512:16], w, src[:, q ^ 8:512:16])
                                                               for w, src, x in terms[1:] for q in range(16)])
            else:
                grps.append([(o, w, src) for w, src, x in terms])
            bk.append("d%d" % i)
        op("p", lambda: mms(grps), r + ["idn", "neg"], bk, bk)

    def banks(n, j, ks):
        i = where[n, j, ks[0]]
        ring.extend(range(i, i + len(ks)))
        return T.psd[:, 512 * i:512 * (i + len(ks))], ["d%d" % (i + y) for y in range(len(ks))]

    def evac(n, j, ks):
        src, bk = banks(n, j, ks)
        op("s", lambda: S.activation(blocks(T["dd%d" % (n % 2)], j, ks), src, AF.Copy), bk, keys("f", n, j, ks), bk)

    def least(n, j, ks, direct=False):
        f = n % 2
        src, r, bk = blocks(T["dd%d" % f], j, ks), keys("f", n, j, ks), []
        if direct:
            src, bk = banks(n, j, ks)
            r = bk
        op("v", lambda: V.tensor_tensor_scan(blocks(T["mm%d" % f], j, ks), T.rst[:, 0:512 * len(ks)], src, 0.0, OP.add, OP.min),
           r + ["rst"], keys("m", n, j, ks), bk)

    def selfs(n):
        f = n % 2
        move(SELF_ON, T["sev%d" % f][:], T["sew%d" % f][:, 0:2048].indirect(T["sel%d" % f][:, 0:16]),
             ["sew%d" % f, "sel%d" % f], ["sev%d" % f])

    G = T.psg
    places = [(k, h) for k in range(4) for h in (0, 1)]

    def sums(n, j):
        f, t = n % 2, n // 2
        m, v = T["mm%d" % f][:, 2048 * j + 7:2048 * j + 2048:8], T["sev%d" % f]
        if t < 2:
            grp = [(G[:, 0:256], T.idn[:], m)]
        else:
            grp = [(G[:, slot_at(t, OWNER[k], h):256:8], T.idn[:], m[:, slice(*gap_cols(t, k, h, 0, 1))]) for k, h in places]
        r = keys("m", n, j, range(4)) + ["idn"]
        if j == 0:
            r += ["sev%d" % f, "neg"]
            if t < 2:
                for k, h in places:
                    a, o = slot_at(t, OWNER[k], h), G[:, slice(*gap_cols(t, k, h, 0, 1))]
                    grp += [(o, T.idn[:], v[:, a:256:8]), (o, T.neg[:], v[:, (a + t + 1) % 8:256:8])]
            else:
                grp = [(G[:, 0:256], T.idn[:], v[:])] + [(G[:, a:256:8], T.neg[:], v[:, (a + 3) % 8:256:8]) for a in range(8)] + grp
        op("p", lambda: mms([grp], start=j == 0, stop=j == 2), r, ["gap"], ["g"])

    def signs(n):
        op("s", lambda: S.activation(T.ind[:], G[:, 0:256], AF.Sign, bias=-0.5), ["gap"], ["ind"], ["g"])

    def count(n):
        t = n // 2
        at = {slot_at(t, OWNER[k], h): (k, h) for k, h in places}
        op("p", lambda: mms([[(T.psm[:, O_CNT:O_CNT + 16], T.bc[:, 15 - q:143 - q],
                               T.ind[:, slice(*gap_cols(t, at[q % 8][0], at[q % 8][1], q // 8, 2))]) for q in range(16)]]),
           ["ind", "bc1"], ["cnt"], ["m"])

    def deaths(n):
        if DEAD_ON == "v":
            op("v", lambda: V.tensor_scalar(T.dead[:], T.psm[:, O_CNT:O_CNT + 16], 15.5, None, OP.is_gt), ["cnt"], ["dead"], ["m"])
        else:
            op("s", lambda: S.activation(T.dead[:], T.psm[:, O_CNT:O_CNT + 16], AF.Relu, bias=-15.0), ["cnt"], ["dead"], ["m"])

    def prefix(n):
        f = n % 2
        hd, key = (T.hd0, "hd0") if n < 2 else (T["hd%d" % (f + 1)], "hd%d" % (f + 1))
        op("p", lambda: mms([[(T.psm[:, O_PRE:O_PRE + 16], T.idn[:], hd[:]), (T.psm[:, O_PRE:O_PRE + 16], T.ltri[:], T.dead[:])]]),
           ["dead", "ltri", key], ["pre"], ["m"])

    def refill(n):
        f = n % 2
        key = "lst%d" % (f + 1)
        old = "lst0" if n < 2 else key
        op("v", lambda: V.tensor_tensor(T[key][:], T.psm[:, O_PRE:O_PRE + 16], T[old][:], OP.max), ["pre", old], [key], ["m"])

    def outgoing(n):
        f = n % 2
        cl = T["call%d" % f]
        op("p", lambda: mms([[(T.psm[:, O_L1 + 32 * b:O_L1 + 32 * b + 32], T.zz[:, 136 * b + 7 - u:136 * b + 135 - u],
                               cl[:, u:256:8]) for u in range(8)] for b in (0, 1)]),
           ["call%d" % f, "zz0", "zz1"], ["l1"], ["m"])

    def heads(n):
        o = T.psm[:, O_HD:O_HD + 16]
        if n < 2:
            op("p", lambda: mms([[(o, T.one8[:], T.dead[:]), (o, T.idn[:], T.hd0[:])]]), ["dead", "one8", "hd0"], ["hdp"], ["m"])

    def heads_out(n):
        if n < 2:
            op("s", lambda: S.activation(T["hd%d" % (n + 1)][:], T.psm[:, O_HD:O_HD + 16], AF.Copy), ["hdp"], ["hd%d" % (n + 1)], ["m"])

    def alive(n):
        op("v", lambda: V.tensor_scalar(T.ind[:], G[:, 0:256], 0.5, 2.0 ** -16, OP.is_lt, OP.subtract), ["gap"], ["ind"], ["g"])

    def living(n):
        op("p", lambda: g.tensor.matmul(T.psm[:, 0:256], T.o16[:], T.ind[:], True, True), ["ind", "o16"], ["liv"], ["m"])

    def gaps_out(n):
        f = n % 2
        yg = T["ygs%d" % f]
        op("s", lambda: S.activation(yg[:], G[:, 0:256], AF.Copy), ["gap"], ["ygs%d" % f], ["g"])
        dmas("dog%d" % f, [("ys"[b * f], T.yg[64 * f:64 * f + 64, 256 * b:256 * b + 256], yg[64 * b:64 * b + 64, :]) for b in (0, 1)],
             reads=["ygs%d" % f])

    def codes_out(n):
        f = n % 2
        yc = T["ycs%d" % f]
        op("v", lambda: V.tensor_tensor(yc[:], T.psm[:, 0:256], T["call%d" % f][:], OP.min), ["liv", "call%d" % f], ["ycs%d" % f], ["m"])
        dmas("doc%d" % f, [("y", T.yc[4 * f:4 * f + 4, 256 * b:256 * b + 256], yc[64 * b:64 * b + 64:16, :]) for b in (0, 1)],
             reads=["ycs%d" % f])

    named = {"ind": signs, "cnt": count, "dead": deaths, "pre": prefix, "fill": refill,
             "call": lambda n: codes(n % 2, T["lst%d" % (n % 2 + 1)], "lst%d" % (n % 2 + 1), CALL_ON), "out": outgoing, "l1": lambda n: l1_out(n + 2, "s"),
             "sel": lambda n: se_list(n % 2), "selc": lambda n: se_list_out(n % 2), "head": heads, "headc": heads_out,
             "c2": c2, "c2c": c2_out, "self": selfs, "alive": alive, "liv": living, "yg": gaps_out, "yc": codes_out}
    by_j = {"s": sums, "p": product}
    by_js = {"y": wrapped, "z": offsets}
    by_block = {"r": raw, "R": lambda n, j, ss: raw(n, j, ss, "v"), "f": fused, "d": diff, "e": evac, "m": least,
                "P": lambda n, j, ks: least(n, j, ks, True)}
    only = {"c2": range(1, 6), "c2c": range(1, 6), "self": range(6), "sel": range(6), "selc": range(6), "head": range(2), "headc": range(2)}
    only.update({w: range(4, 6) for w in ("alive", "liv", "yg", "yc")})
    for n in range(-2, 8):
        for w in ORDER.get(n, ORDER.get("all", "")).split():
            m = n + w.count("+") - w.count("-")
            w = w.rstrip("+-")
            if m not in (only.get(w, range(4)) if w in named else range(6)):
                continue
            if w in named:
                named[w](m)
            elif w[0] in by_j:
                by_j[w[0]](m, int(w[1:]))
            elif w[0] in by_js:
                by_js[w[0]](m, [int(c) for c in w[1:]])
            else:
                by_block[w[0]](m, int(w[1]), [int(c) for c in w[2:]])

    for sem in total:
        if max(seen[q].get(sem, 0) for q in Q) < total[sem]:
            need("g", (sem, total[sem]))
